import numpy as np
import ml_dtypes


def mxq(x, axis, fmt="e4m3"):
    dtype, down = {"e4m3": (ml_dtypes.float8_e4m3fn, 7), "e5m2": (ml_dtypes.float8_e5m2, 14)}[fmt]
    v = np.moveaxis(np.asarray(x, np.float32).astype(ml_dtypes.bfloat16).astype(np.float64), axis, -1)
    blocks = v.reshape(v.shape[:-1] + (-1, 32))
    amax = np.abs(blocks).max(-1, keepdims=True)
    byte = np.maximum(np.where(amax > 0, np.frexp(amax)[1] - 1 + 127, 0) - down, 1)
    scale = np.exp2(byte - 127.0)
    codes = (blocks / scale).astype(np.float32).astype(dtype).astype(np.float64)
    return np.moveaxis((codes * scale).reshape(v.shape), -1, axis)


WIDE = False


def mx_kscale(k):
    if not WIDE:
        return np.ones(k)
    levels = np.array([10, -10, 5, -5, 0])
    if k % 512:
        return np.exp2(np.random.permutation(np.resize(levels, k // 32))).repeat(32)
    a = np.empty((k // 512, 16))
    for p in range(k // 512):
        a[p, :8] = np.random.permutation(np.resize(levels, 8))
        for g in range(8):
            far = levels[np.abs(levels - a[p, g]) >= 10]
            a[p, g + 8] = far[np.random.randint(len(far))]
    return np.exp2(a.ravel()).repeat(32)


BF16 = ml_dtypes.bfloat16


def bf(x):
    return np.asarray(x, np.float32).astype(BF16)


def f64(x):
    return np.asarray(x).astype(np.float64)


B, T, A, E = 2, 1024, 256, 512
F = 2 * A
EPS = 1e-6


def dpfp_features(x):
    p = np.maximum(np.concatenate([x, -x], axis=-1), 0.0)
    r = p * np.roll(p, 1, axis=-1)
    return r / np.sqrt(np.mean(r * r, axis=-1, keepdims=True) + EPS)


def draw0():
    t = mx_kscale(T)
    u = mx_kscale(F)
    return {
        "q": bf(np.random.standard_normal((B, T, A)) * 0.08),
        "k": bf(np.random.standard_normal((B, T, A)) * 0.08),
        "v": bf(np.random.standard_normal((B, T, E)) / t[None, :, None]),
        "beta": bf(np.random.standard_normal((B, T)) * t[None, :]),
        "s0": bf(np.random.standard_normal((B, F, E))),
        "gq": bf(np.random.standard_normal(F) * u),
        "gs": bf((1.0 + 0.1 * np.random.standard_normal(F)) / u),
    }


def core(q, k, v, beta, s0, gq, gs):
    t_len = k.shape[1]
    f_dim = s0.shape[1]
    kw = dpfp_features(f64(k)) * f64(beta)[:, :, None]
    d = (mxq(kw, 1, "e4m3").transpose(0, 2, 1) @ mxq(f64(v), 1, "e4m3")) / np.sqrt(t_len)
    s = (0.7 * f64(s0) + d) * f64(gs)[None, :, None]
    qf = dpfp_features(f64(q)) * f64(gq)[None, None, :]
    return (mxq(qf, 2, "e4m3") @ mxq(s, 1, "e4m3")) / np.sqrt(f_dim)


def e4m3fn_bytes(y):
    return np.clip(np.asarray(y, np.float64), -448.0, 448.0).astype(np.float32).astype(ml_dtypes.float8_e4m3fn).view(np.uint8)


def e4m3fn_values(b):
    return np.asarray(b, np.uint8).view(ml_dtypes.float8_e4m3fn).astype(np.float64)


def setup_inputs():
    d = draw0()
    x0 = np.asarray(d['v']).astype(np.float64)
    s = (np.max(np.abs(x0), axis=(0, 2), keepdims=True) / 448.0).astype(np.float32)
    out = {}
    for k, v in d.items():
        if k == 'v':
            out['v_bytes'] = e4m3fn_bytes(x0 / s.astype(np.float64))
            out['v_scale'] = s
        else:
            out[k] = v
    return out


def reference(q, k, v_bytes, v_scale, beta, s0, gq, gs):
    return core(q, k, e4m3fn_values(v_bytes) * v_scale.astype(np.float64), beta, s0, gq, gs)

@@ -1,0 +1,255 @@
+from contextlib import ExitStack
+
+import concourse.mybir as mybir
+from concourse.masks import make_identity
+
+B, T, A, E = 2, 1024, 256, 512
+F = 2 * A
+P = 128
+J = 4
+GT = P * J
+G = T // GT
+
+F32 = mybir.dt.float32
+BF16 = mybir.dt.bfloat16
+U32 = mybir.dt.uint32
+U8 = mybir.dt.uint8
+F8 = mybir.dt.float8_e4m3fn
+X4 = mybir.dt.float8_e4m3fn_x4
+ALU = mybir.AluOpType
+ACT = mybir.ActivationFunctionType
+
+FLOPS = 2 * 2 * B * T * F * E
+
+
+def tile_dpfpfastweightwriteread_kernel(tc, q, k, v_bytes, v_scale, beta, s0, gq, gs, out):
+    nc = tc.nc
+
+    with ExitStack() as ctx:
+        const = ctx.enter_context(tc.tile_pool(name="const", bufs=1))
+        loads = ctx.enter_context(tc.tile_pool(name="loads", bufs=1))
+        work = ctx.enter_context(tc.tile_pool(name="work", bufs=3))
+        codes = ctx.enter_context(tc.tile_pool(name="codes", bufs=3))
+        psum_d = ctx.enter_context(tc.psum_pool(name="psum_d", bufs=1))
+        psum_o = ctx.enter_context(tc.psum_pool(name="psum_o", bufs=2))
+        psum_t = ctx.enter_context(tc.psum_pool(name="psum_t", bufs=2))
+
+        xk, xq, vb, s0r = {}, {}, {}, {}
+
+        def load_x(src, b, g, name):
+            t = loads.tile([P, J, A], BF16, name=name)
+            nc.sync.dma_start(out=t[:], in_=src[b].rearrange("(g p j) a -> g p j a", p=P, j=J)[g])
+            return t
+
+        def load_v(b, g):
+            t = loads.tile([P, J, E], U8, name=f"vb{b}{g}")
+            nc.sync.dma_start(out=t[:], in_=v_bytes[b].rearrange("(g p j) e -> g p j e", p=P, j=J)[g])
+            return t
+
+        def load_s0(b):
+            t = loads.tile([P, J, E], BF16, name=f"s0{b}")
+            nc.sync.dma_start(out=t[:], in_=s0[b].rearrange("(p j) e -> p j e", j=J))
+            return t
+
+        beta_r = const.tile([P, B * G, J], BF16, name="beta_r")
+        nc.scalar.dma_start(out=beta_r[:], in_=beta.rearrange("b t -> (b t)").rearrange("(n p j) -> p n j", p=P, j=J))
+        vs_r = const.tile([P, G, J], F32, name="vs_r")
+        nc.scalar.dma_start(out=vs_r[:], in_=v_scale.rearrange("o t u -> (o t u)").rearrange("(n p j) -> p n j", p=P, j=J))
+        gs_r = const.tile([P, J], BF16, name="gs_r")
+        nc.scalar.dma_start(out=gs_r[:], in_=gs.rearrange("(p j) -> p j", j=J))
+
+        for b in range(B):
+            for g in range(G):
+                xk[b, g] = load_x(k, b, g, f"xk{b}{g}")
+                vb[b, g] = load_v(b, g)
+            if b == 0:
+                gq_t = const.tile([P, F], BF16, name="gq_t")
+                nc.sync.dma_start(out=gq_t[:], in_=gq.partition_broadcast(P))
+            xq[b, 0] = load_x(q, b, 0, f"xq{b}0")
+            s0r[b] = load_s0(b)
+            xq[b, 1] = load_x(q, b, 1, f"xq{b}1")
+
+        ident = const.tile([P, P], F32, name="ident")
+        make_identity(nc, ident[:])
+
+        one = const.tile([P, 1], F32, name="one")
+        nc.vector.memset(one[:], 1.0)
+        eps = const.tile([P, 1], F32, name="eps")
+        nc.vector.tensor_scalar(out=eps[:], in0=one[:], scalar1=2.5e-7, scalar2=None, op0=ALU.mult)
+        absb = const.tile([P, B * G, J], F32, name="absb")
+        nc.vector.scalar_tensor_tensor(out=absb[:], in0=beta_r[:], scalar=-1.0, in1=beta_r[:], op0=ALU.mult, op1=ALU.max)
+        sgn = const.tile([P, B, G * J], F32, name="sgn")
+        nc.vector.tensor_scalar(
+            out=sgn[:].rearrange("p b (g j) -> p (b g) j", j=J), in0=beta_r[:], scalar1=0.0, scalar2=0.5, op0=ALU.is_ge, op1=ALU.subtract
+        )
+        vss = const.tile([P, B, G * J], F32, name="vss")
+        nc.vector.scalar_tensor_tensor(
+            out=vss[:],
+            in0=sgn[:],
+            scalar=2.0,
+            in1=vs_r[:].rearrange("p g j -> p (g j)").unsqueeze(1).to_broadcast([P, B, G * J]),
+            op0=ALU.mult,
+            op1=ALU.mult,
+        )
+        g07 = const.tile([P, J], F32, name="g07")
+        nc.vector.tensor_scalar(out=g07[:], in0=gs_r[:], scalar1=0.7, scalar2=None, op0=ALU.mult)
+        gs32 = const.tile([P, J], F32, name="gs32")
+        nc.vector.tensor_scalar(out=gs32[:], in0=gs_r[:], scalar1=1.0 / 32.0, scalar2=None, op0=ALU.mult)
+
+        def front(x, absb_n):
+            h = work.tile([P, J, A], BF16, name="h")
+            nc.vector.tensor_scalar(out=h[:], in0=x[:], scalar1=0.0, scalar2=0.5, op0=ALU.is_ge, op1=ALU.subtract)
+            w = work.tile([P, J, A], BF16, name="w")
+            nc.vector.tensor_tensor(out=w[:, :, 1:A], in0=h[:, :, 1:A], in1=x[:, :, 0 : A - 1], op=ALU.mult)
+            nc.vector.scalar_tensor_tensor(
+                out=w[:, :, 0:1], in0=x[:, :, A - 1 : A], scalar=-1.0, in1=h[:, :, 0:1], op0=ALU.mult, op1=ALU.mult
+            )
+            z = work.tile([P, J, A], F32, name="z")
+            nc.vector.scalar_tensor_tensor(out=z[:], in0=w[:], scalar=0.0, in1=x[:], op0=ALU.max, op1=ALU.mult)
+            ss = work.tile([P, J], F32, name="ss")
+            for t in range(J):
+                junk = work.tile([P, A], BF16, name="junk")
+                nc.scalar.activation(out=junk[:], in_=z[:, t, :], func=ACT.Square, accum_out=ss[:, t : t + 1])
+            rt = work.tile([P, J], F32, name="rt")
+            nc.scalar.activation(out=rt[:], in_=ss[:], func=ACT.Sqrt, scale=1.0 / 512.0, bias=eps[:])
+            inv = work.tile([P, J], F32, name="inv")
+            nc.vector.reciprocal(out=inv[:], in_=rt[:])
+            if absb_n is None:
+                return z, inv
+            sk = work.tile([P, J], F32, name="sk")
+            nc.vector.tensor_tensor(out=sk[:], in0=inv[:], in1=absb_n, op=ALU.mult)
+            return z, sk
+
+        def quantize(src, name):
+            c = codes.tile([P, GT], U32, align_bytes=64, name=name + "c")
+            s = codes.tile([P, GT], U8, align_bytes=64, name=name + "s")
+            nc.vector.quantize_mx(out=c[:].bitcast(X4), scales=s[:], in_=src)
+            return c, s
+
+        def interleave(dst, src):
+            nc.vector.tensor_copy(out=dst, in_=src.rearrange("p t n -> p n t"))
+
+        def k_back(z, sk):
+            zs = work.tile([P, J, A], BF16, name="zs")
+            for t in range(J):
+                nc.scalar.activation(
+                    out=zs[:, t, :].rearrange("p (j m) -> p j m", j=4),
+                    in_=z[:, t, :].rearrange("p (m j) -> p j m", j=4),
+                    func=ACT.Copy,
+                    scale=sk[:, t : t + 1],
+                )
+            zi = work.tile([P, A, J], BF16, name="zi")
+            interleave(zi[:], zs[:])
+            kw = work.tile([P, F, J], BF16, align_bytes=64, name="kw")
+            kwv = kw[:].rearrange("p (j h m) t -> p h j (m t)", j=4, h=2)
+            ziv = zi[:].rearrange("p (j m) t -> p j (m t)", j=4)
+            nc.vector.tensor_scalar(out=kwv[:, 0], in0=ziv, scalar1=0.0, scalar2=None, op0=ALU.max)
+            nc.vector.tensor_scalar(out=kwv[:, 1], in0=ziv, scalar1=-1.0, scalar2=0.0, op0=ALU.mult, op1=ALU.max)
+            return quantize(kw[:].rearrange("p n t -> p (n t)"), "kw")
+
+        def v_all(b, g):
+            vw = work.tile([P, J, E], BF16, name="vw")
+            for t in range(J):
+                nc.scalar.activation(
+                    out=vw[:, t, :],
+                    in_=vb[b, g][:, t, :].bitcast(F8),
+                    func=ACT.Copy,
+                    scale=vss[:, b, g * J + t : g * J + t + 1],
+                )
+            vi = work.tile([P, E, J], BF16, align_bytes=64, name="vi")
+            interleave(vi[:], vw[:])
+            return quantize(vi[:].rearrange("p n t -> p (n t)"), "v")
+
+        def q_mid(z, inv):
+            y = work.tile([P, J, A], F32, name="y")
+            for t in range(J):
+                nc.scalar.activation(out=y[:, t, :], in_=z[:, t, :], func=ACT.Copy, scale=inv[:, t : t + 1])
+            qf = work.tile([P, J, F], BF16, name="qf")
+            for h, op in ((0, ALU.max), (1, ALU.min)):
+                cols = slice(h * A, (h + 1) * A)
+                nc.vector.scalar_tensor_tensor(
+                    out=qf[:, :, cols],
+                    in0=y[:],
+                    scalar=0.0,
+                    in1=gq_t[:, cols].unsqueeze(1).to_broadcast([P, J, A]),
+                    op0=op,
+                    op1=ALU.mult,
+                )
+            words = qf[:].bitcast(F32)
+            qg = work.tile([P, J * P * 4], BF16, align_bytes=64, name="qg")
+            qgw = qg[:].bitcast(F32)
+            for h in range(2):
+                tr = psum_t.tile([P, 2, 2, P], F32, name="tr")
+                for a in range(2):
+                    for u in range(2):
+                        nc.tensor.transpose(tr[:, a, u, :], words[:, 2 * h + a, u : F // 2 : 2], ident[:])
+                nc.scalar.copy(
+                    out=qgw[:, h * 512 : (h + 1) * 512].rearrange("p (a r u) -> p a r u", a=2, u=2),
+                    in_=tr[:].rearrange("p a u r -> p a r u"),
+                )
+            return quantize(qg[:], "q")
+
+        def write(b, kv):
+            d = [psum_d.tile([P, E], F32, name=f"d{j}") for j in range(4)]
+            for g in range(G):
+                (kc, ks), (vc, vs) = kv[g]
+                for j in range(4):
+                    cols = slice(128 * j, 128 * (j + 1))
+                    nc.tensor.matmul_mx(
+                        out=d[j][:],
+                        lhsT=kc[:, cols].bitcast(X4),
+                        lhsT_scale=ks[:, cols],
+                        rhs=vc[:].bitcast(X4),
+                        rhs_scale=vs[:],
+                        start=(g == 0),
+                        stop=(g == G - 1),
+                    )
+            return d
+
+        def state(b, d):
+            s0g = work.tile([P, 4, E], F32, name="s0g")
+            sp = work.tile([P, 4, E], BF16, name="sp")
+            for j in range(4):
+                nc.scalar.activation(out=s0g[:, j, :], in_=s0r[b][:, j, :], func=ACT.Copy, scale=g07[:, j : j + 1])
+            for j in range(4):
+                nc.vector.scalar_tensor_tensor(
+                    out=sp[:, j, :], in0=d[j][:], scalar=gs32[:, j : j + 1], in1=s0g[:, j, :], op0=ALU.mult, op1=ALU.add
+                )
+            si = work.tile([P, E, 4], BF16, align_bytes=64, name="si")
+            interleave(si[:], sp[:])
+            return quantize(si[:].rearrange("p n t -> p (n t)"), "s")
+
+        def read(b, g, qq, sq):
+            (qc, qs), (sc, ss) = qq, sq
+            ov = out[b].rearrange("(g p j) e -> g p j e", p=P, j=J)[g]
+            for h in range(2):
+                ot = work.tile([P, 2, E], F32, name="ot")
+                for a in range(2):
+                    cols = slice(128 * (2 * h + a), 128 * (2 * h + a + 1))
+                    o = psum_o.tile([P, E], F32, name="o")
+                    nc.tensor.matmul_mx(
+                        out=o[:],
+                        lhsT=qc[:, cols].bitcast(X4),
+                        lhsT_scale=qs[:, cols],
+                        rhs=sc[:].bitcast(X4),
+                        rhs_scale=ss[:],
+                        start=True,
+                        stop=True,
+                    )
+                    nc.scalar.activation(out=ot[:, a, :], in_=o[:], func=ACT.Copy, scale=512.0**-0.5)
+                nc.sync.dma_start(out=ov[:, 2 * h : 2 * h + 2, :], in_=ot[:])
+
+        nc.vector.tensor_scalar(out=gq_t[:, A:F], in0=gq_t[:, A:F], scalar1=-1.0, scalar2=None, op0=ALU.mult)
+        for b in range(B):
+            zk = [front(xk[b, g], absb[:, b * G + g, :]) for g in range(G)]
+            vq = []
+            kq = []
+            for g in range(G):
+                vq.append(v_all(b, g))
+                kq.append(k_back(zk[g][0], zk[g][1]))
+            zq = [front(xq[b, g], None) for g in range(G)]
+            d = write(b, [(kq[g], vq[g]) for g in range(G)])
+            sq = state(b, d)
+            qm = [q_mid(zq[g][0], zq[g][1]) for g in range(G)]
+            for g in range(G):
+                read(b, g, qm[g], sq)

@@ -18,6 +18,11 @@ F8 = mybir.dt.float8_e4m3fn
 X4 = mybir.dt.float8_e4m3fn_x4
 ALU = mybir.AluOpType
 ACT = mybir.ActivationFunctionType
+I32 = mybir.dt.int32
+SIGNS = -0x7FFF8000
+SHIFT_SCALAR = {("k", 0, 0)}
+Y_VECTOR = {("q", 0, 1), ("q", 1, 1)}
+EVAC_VECTOR = {(("q", 1, 1), 1, 1), (("q", 1, 1), 0, 1)}
 
 FLOPS = 2 * 2 * B * T * F * E
 
@@ -29,27 +34,45 @@ def tile_dpfpfastweightwriteread_kernel(tc, q, k, v_bytes, v_scale, beta, s0, gq
         const = ctx.enter_context(tc.tile_pool(name="const", bufs=1))
         loads = ctx.enter_context(tc.tile_pool(name="loads", bufs=1))
         work = ctx.enter_context(tc.tile_pool(name="work", bufs=3))
+        outs = ctx.enter_context(tc.tile_pool(name="outs", bufs=5))
+        zpool = ctx.enter_context(tc.tile_pool(name="zpool", bufs=4))
         codes = ctx.enter_context(tc.tile_pool(name="codes", bufs=3))
         psum_d = ctx.enter_context(tc.psum_pool(name="psum_d", bufs=1))
         psum_o = ctx.enter_context(tc.psum_pool(name="psum_o", bufs=2))
         psum_t = ctx.enter_context(tc.psum_pool(name="psum_t", bufs=2))
 
-        xk, xq, vb, s0r = {}, {}, {}, {}
+        x_t, xn_t, vb, s0r = {}, {}, {}, {}
 
-        def load_x(src, b, g, name):
-            t = loads.tile([P, J, A], BF16, name=name)
-            nc.sync.dma_start(out=t[:], in_=src[b].rearrange("(g p j) a -> g p j a", p=P, j=J)[g])
-            return t
+        def load_x(kind, b, g):
+            src = k if kind == "k" else q
+            flat = src.rearrange("b t a -> (b t a)")
+            size = GT * A
+            base = (b * G + g) * size
+            row = J * A
+            x = loads.tile([P, J, A], BF16, name=f"x{kind}{b}{g}")
+            nc.sync.dma_start(out=x[:], in_=src[b].rearrange("(g p j) a -> g p j a", p=P, j=J)[g])
+            xn = loads.tile([P, J, A], BF16, name=f"xn{kind}{b}{g}")
+            xnf = xn[:].rearrange("p j a -> p (j a)")
+            if (kind, b, g) in SHIFT_SCALAR:
+                nc.scalar.copy(out=xnf[:, 0 : row - 1], in_=x[:].rearrange("p j a -> p (j a)")[:, 1:row])
+            elif base + size < B * T * A:
+                nc.sync.dma_start(out=xnf, in_=flat[base + 1 : base + 1 + size].rearrange("(p f) -> p f", f=row))
+            else:
+                cut = base + 1 + (P - 1) * row
+                nc.sync.dma_start(out=xnf[0 : P - 1], in_=flat[base + 1 : cut].rearrange("(p f) -> p f", f=row))
+                nc.sync.dma_start(out=xnf[P - 1 : P, 0 : row - 1], in_=flat[cut : base + size].unsqueeze(0))
+            x_t[kind, b, g] = x
+            xn_t[kind, b, g] = xn
 
         def load_v(b, g):
             t = loads.tile([P, J, E], U8, name=f"vb{b}{g}")
             nc.sync.dma_start(out=t[:], in_=v_bytes[b].rearrange("(g p j) e -> g p j e", p=P, j=J)[g])
-            return t
+            vb[b, g] = t
 
         def load_s0(b):
             t = loads.tile([P, J, E], BF16, name=f"s0{b}")
             nc.sync.dma_start(out=t[:], in_=s0[b].rearrange("(p j) e -> p j e", j=J))
-            return t
+            s0r[b] = t
 
         beta_r = const.tile([P, B * G, J], BF16, name="beta_r")
         nc.scalar.dma_start(out=beta_r[:], in_=beta.rearrange("b t -> (b t)").rearrange("(n p j) -> p n j", p=P, j=J))
@@ -58,16 +81,17 @@ def tile_dpfpfastweightwriteread_kernel(tc, q, k, v_bytes, v_scale, beta, s0, gq
         gs_r = const.tile([P, J], BF16, name="gs_r")
         nc.scalar.dma_start(out=gs_r[:], in_=gs.rearrange("(p j) -> p j", j=J))
 
+        gq_t = const.tile([P, F], BF16, name="gq_t")
         for b in range(B):
             for g in range(G):
-                xk[b, g] = load_x(k, b, g, f"xk{b}{g}")
-                vb[b, g] = load_v(b, g)
-            if b == 0:
-                gq_t = const.tile([P, F], BF16, name="gq_t")
-                nc.sync.dma_start(out=gq_t[:], in_=gq.partition_broadcast(P))
-            xq[b, 0] = load_x(q, b, 0, f"xq{b}0")
-            s0r[b] = load_s0(b)
-            xq[b, 1] = load_x(q, b, 1, f"xq{b}1")
+                load_x("k", b, g)
+                load_v(b, g)
+            load_s0(b)
+        for b in range(B):
+            for g in range(G):
+                load_x("q", b, g)
+                if b + g == 0:
+                    nc.sync.dma_start(out=gq_t[:], in_=gq.partition_broadcast(P))
 
         ident = const.tile([P, P], F32, name="ident")
         make_identity(nc, ident[:])
@@ -75,7 +99,7 @@ def tile_dpfpfastweightwriteread_kernel(tc, q, k, v_bytes, v_scale, beta, s0, gq
         one = const.tile([P, 1], F32, name="one")
         nc.vector.memset(one[:], 1.0)
         eps = const.tile([P, 1], F32, name="eps")
-        nc.vector.tensor_scalar(out=eps[:], in0=one[:], scalar1=2.5e-7, scalar2=None, op0=ALU.mult)
+        nc.vector.tensor_scalar(out=eps[:], in0=one[:], scalar1=1e-6, scalar2=None, op0=ALU.mult)
         absb = const.tile([P, B * G, J], F32, name="absb")
         nc.vector.scalar_tensor_tensor(out=absb[:], in0=beta_r[:], scalar=-1.0, in1=beta_r[:], op0=ALU.mult, op1=ALU.max)
         sgn = const.tile([P, B, G * J], F32, name="sgn")
@@ -91,45 +115,87 @@ def tile_dpfpfastweightwriteread_kernel(tc, q, k, v_bytes, v_scale, beta, s0, gq
             op0=ALU.mult,
             op1=ALU.mult,
         )
-        g07 = const.tile([P, J], F32, name="g07")
-        nc.vector.tensor_scalar(out=g07[:], in0=gs_r[:], scalar1=0.7, scalar2=None, op0=ALU.mult)
         gs32 = const.tile([P, J], F32, name="gs32")
         nc.vector.tensor_scalar(out=gs32[:], in0=gs_r[:], scalar1=1.0 / 32.0, scalar2=None, op0=ALU.mult)
+        dgs = const.tile([P, J, P], F32, name="dgs")
+        gqn = const.tile([P, A], BF16, name="gqn")
+        st = {}
 
-        def front(x, absb_n):
-            h = work.tile([P, J, A], BF16, name="h")
-            nc.vector.tensor_scalar(out=h[:], in0=x[:], scalar1=0.0, scalar2=0.5, op0=ALU.is_ge, op1=ALU.subtract)
-            w = work.tile([P, J, A], BF16, name="w")
-            nc.vector.tensor_tensor(out=w[:, :, 1:A], in0=h[:, :, 1:A], in1=x[:, :, 0 : A - 1], op=ALU.mult)
-            nc.vector.scalar_tensor_tensor(
-                out=w[:, :, 0:1], in0=x[:, :, A - 1 : A], scalar=-1.0, in1=h[:, :, 0:1], op0=ALU.mult, op1=ALU.mult
+        def cd():
+            for j in range(J):
+                nc.gpsimd.tensor_scalar(
+                    out=dgs[:, j, :], in0=ident[:], scalar1=gs32[:, j : j + 1], scalar2=0.0, op0=ALU.mult, op1=ALU.add
+                )
+
+        def cg():
+            nc.gpsimd.tensor_scalar(out=gqn[:], in0=gq_t[:, A:F], scalar1=-1.0, scalar2=0.0, op0=ALU.mult, op1=ALU.add)
+
+        def xn(u):
+            nc.gpsimd.tensor_scalar(
+                out=xn_t[u][:, :, A - 1 : A], in0=x_t[u][:, :, 0:1], scalar1=-1.0, scalar2=None, op0=ALU.mult
             )
-            z = work.tile([P, J, A], F32, name="z")
-            nc.vector.scalar_tensor_tensor(out=z[:], in0=w[:], scalar=0.0, in1=x[:], op0=ALU.max, op1=ALU.mult)
+
+        def xw(u):
+            x, xs_ = x_t[u], xn_t[u]
+            w = work.tile([P, J, A], BF16, name="w")
+            nc.vector.scalar_tensor_tensor(
+                out=w[:].rearrange("p j a -> p (j a)").bitcast(I32),
+                in0=xs_[:].rearrange("p j a -> p (j a)").bitcast(I32),
+                scalar=SIGNS,
+                in1=x[:].rearrange("p j a -> p (j a)").bitcast(I32),
+                op0=ALU.bitwise_and,
+                op1=ALU.bitwise_xor,
+            )
+            st["w", u] = w
+
+        def xz(u):
+            x, w = x_t[u], st["w", u]
+            z = zpool.tile([P, J, A], F32, name="z")
+            nc.vector.scalar_tensor_tensor(
+                out=z[:, :, 1:A], in0=w[:, :, 0 : A - 1], scalar=0.0, in1=x[:, :, 1:A], op0=ALU.max, op1=ALU.mult
+            )
+            nc.vector.scalar_tensor_tensor(
+                out=z[:, :, 0:1], in0=w[:, :, A - 1 : A], scalar=0.0, in1=x[:, :, 0:1], op0=ALU.max, op1=ALU.mult
+            )
+            st["z", u] = z
+
+        def xs(u):
+            z = st["z", u]
             ss = work.tile([P, J], F32, name="ss")
             for t in range(J):
                 junk = work.tile([P, A], BF16, name="junk")
                 nc.scalar.activation(out=junk[:], in_=z[:, t, :], func=ACT.Square, accum_out=ss[:, t : t + 1])
             rt = work.tile([P, J], F32, name="rt")
             nc.scalar.activation(out=rt[:], in_=ss[:], func=ACT.Sqrt, scale=1.0 / 512.0, bias=eps[:])
-            inv = work.tile([P, J], F32, name="inv")
-            nc.vector.reciprocal(out=inv[:], in_=rt[:])
-            if absb_n is None:
-                return z, inv
-            sk = work.tile([P, J], F32, name="sk")
-            nc.vector.tensor_tensor(out=sk[:], in0=inv[:], in1=absb_n, op=ALU.mult)
-            return z, sk
+            st["rt", u] = rt
 
-        def quantize(src, name):
-            c = codes.tile([P, GT], U32, align_bytes=64, name=name + "c")
-            s = codes.tile([P, GT], U8, align_bytes=64, name=name + "s")
+        def xr(u):
+            kind, b, g = u
+            inv = zpool.tile([P, J], F32, name="inv")
+            nc.vector.reciprocal(out=inv[:], in_=st["rt", u][:])
+            st["inv", u] = inv
+
+        def xm(u):
+            kind, b, g = u
+            if kind == "k":
+                inv = st["inv", u]
+                sk = zpool.tile([P, J], F32, name="sk")
+                nc.gpsimd.tensor_tensor(out=sk[:], in0=inv[:], in1=absb[:, b * G + g, :], op=ALU.mult)
+                st["inv", u] = sk
+
+        def quantize(src, name, width=GT):
+            c = codes.tile([P, width], U32, align_bytes=64, name=name + "c")
+            s = codes.tile([P, width], U8, align_bytes=64, name=name + "s")
             nc.vector.quantize_mx(out=c[:].bitcast(X4), scales=s[:], in_=src)
             return c, s
 
         def interleave(dst, src):
-            nc.vector.tensor_copy(out=dst, in_=src.rearrange("p t n -> p n t"))
+            nc.vector.tensor_copy(
+                out=dst.rearrange("p (c i) t -> p c t i", i=4), in_=src.rearrange("p t (c i) -> p c t i", i=4)
+            )
 
-        def k_back(z, sk):
+        def kz(u):
+            z, sk = st["z", u], st["inv", u]
             zs = work.tile([P, J, A], BF16, name="zs")
             for t in range(J):
                 nc.scalar.activation(
@@ -138,118 +204,337 @@ def tile_dpfpfastweightwriteread_kernel(tc, q, k, v_bytes, v_scale, beta, s0, gq
                     func=ACT.Copy,
                     scale=sk[:, t : t + 1],
                 )
+            st["zs", u] = zs
+
+        def ki(u):
             zi = work.tile([P, A, J], BF16, name="zi")
-            interleave(zi[:], zs[:])
+            interleave(zi[:], st["zs", u][:])
+            st["zi", u] = zi
+
+        def kh(u):
             kw = work.tile([P, F, J], BF16, align_bytes=64, name="kw")
             kwv = kw[:].rearrange("p (j h m) t -> p h j (m t)", j=4, h=2)
-            ziv = zi[:].rearrange("p (j m) t -> p j (m t)", j=4)
+            ziv = st["zi", u][:].rearrange("p (j m) t -> p j (m t)", j=4)
             nc.vector.tensor_scalar(out=kwv[:, 0], in0=ziv, scalar1=0.0, scalar2=None, op0=ALU.max)
             nc.vector.tensor_scalar(out=kwv[:, 1], in0=ziv, scalar1=-1.0, scalar2=0.0, op0=ALU.mult, op1=ALU.max)
-            return quantize(kw[:].rearrange("p n t -> p (n t)"), "kw")
+            st["kw", u] = kw
 
-        def v_all(b, g):
-            vw = work.tile([P, J, E], BF16, name="vw")
+        def kq(u):
+            st["kc", u] = quantize(st["kw", u][:].rearrange("p n t -> p (n t)"), "kw")
+
+        def vw(b, g):
+            t_ = work.tile([P, J, E], BF16, name="vw")
             for t in range(J):
                 nc.scalar.activation(
-                    out=vw[:, t, :],
+                    out=t_[:, t, :],
                     in_=vb[b, g][:, t, :].bitcast(F8),
                     func=ACT.Copy,
                     scale=vss[:, b, g * J + t : g * J + t + 1],
                 )
-            vi = work.tile([P, E, J], BF16, align_bytes=64, name="vi")
-            interleave(vi[:], vw[:])
-            return quantize(vi[:].rearrange("p n t -> p (n t)"), "v")
+            st["vw", b, g] = t_
 
-        def q_mid(z, inv):
+        def vi(b, g):
+            t_ = work.tile([P, E, J], BF16, align_bytes=64, name="vi")
+            interleave(t_[:], st["vw", b, g][:])
+            st["vi", b, g] = t_
+
+        def vq(b, g):
+            st["vc", b, g] = quantize(st["vi", b, g][:].rearrange("p n t -> p (n t)"), "v")
+
+        def qy(u):
             y = work.tile([P, J, A], F32, name="y")
             for t in range(J):
-                nc.scalar.activation(out=y[:, t, :], in_=z[:, t, :], func=ACT.Copy, scale=inv[:, t : t + 1])
-            qf = work.tile([P, J, F], BF16, name="qf")
-            for h, op in ((0, ALU.max), (1, ALU.min)):
-                cols = slice(h * A, (h + 1) * A)
+                if u in Y_VECTOR:
+                    nc.vector.tensor_scalar(
+                        out=y[:, t, :], in0=st["z", u][:, t, :], scalar1=st["inv", u][:, t : t + 1], scalar2=None, op0=ALU.mult
+                    )
+                else:
+                    nc.scalar.activation(out=y[:, t, :], in_=st["z", u][:, t, :], func=ACT.Copy, scale=st["inv", u][:, t : t + 1])
+            st["y", u] = y
+
+        def qg(u, hh):
+            y = st["y", u]
+            qf = work.tile([P, 2, F], BF16, name="qf")
+            t0, t1 = 2 * hh, 2 * hh + 2
+            st["qf", u, hh] = qf
+            for h, op, gain in ((0, ALU.max, gq_t[:, 0:A]), (1, ALU.min, gqn[:])):
                 nc.vector.scalar_tensor_tensor(
-                    out=qf[:, :, cols],
-                    in0=y[:],
+                    out=qf[:, :, h * A : (h + 1) * A],
+                    in0=y[:, t0:t1, :],
                     scalar=0.0,
-                    in1=gq_t[:, cols].unsqueeze(1).to_broadcast([P, J, A]),
+                    in1=gain.unsqueeze(1).to_broadcast([P, t1 - t0, A]),
                     op0=op,
                     op1=ALU.mult,
                 )
-            words = qf[:].bitcast(F32)
-            qg = work.tile([P, J * P * 4], BF16, align_bytes=64, name="qg")
-            qgw = qg[:].bitcast(F32)
-            for h in range(2):
-                tr = psum_t.tile([P, 2, 2, P], F32, name="tr")
-                for a in range(2):
-                    for u in range(2):
-                        nc.tensor.transpose(tr[:, a, u, :], words[:, 2 * h + a, u : F // 2 : 2], ident[:])
-                nc.scalar.copy(
-                    out=qgw[:, h * 512 : (h + 1) * 512].rearrange("p (a r u) -> p a r u", a=2, u=2),
-                    in_=tr[:].rearrange("p a u r -> p a r u"),
-                )
-            return quantize(qg[:], "q")
 
-        def write(b, kv):
-            d = [psum_d.tile([P, E], F32, name=f"d{j}") for j in range(4)]
-            for g in range(G):
-                (kc, ks), (vc, vs) = kv[g]
-                for j in range(4):
-                    cols = slice(128 * j, 128 * (j + 1))
-                    nc.tensor.matmul_mx(
-                        out=d[j][:],
-                        lhsT=kc[:, cols].bitcast(X4),
-                        lhsT_scale=ks[:, cols],
-                        rhs=vc[:].bitcast(X4),
-                        rhs_scale=vs[:],
-                        start=(g == 0),
-                        stop=(g == G - 1),
-                    )
-            return d
+        def qt(u, h):
+            words = st["qf", u, h][:].bitcast(F32)
+            tr = psum_t.tile([P, 2, 2, P], F32, name="tr")
+            for a in range(2):
+                for c in range(2):
+                    nc.tensor.transpose(tr[:, a, c, :], words[:, a, c : F // 2 : 2], ident[:])
+            st["tr", u, h] = tr
 
-        def state(b, d):
-            s0g = work.tile([P, 4, E], F32, name="s0g")
-            sp = work.tile([P, 4, E], BF16, name="sp")
+        def qe(u, h):
+            tr = st["tr", u, h]
+            qw = work.tile([P, 2 * P * 4], BF16, align_bytes=64, name="qw")
+            nc.scalar.copy(
+                out=qw[:].bitcast(F32).rearrange("p (a r c) -> p a r c", a=2, c=2),
+                in_=tr[:].rearrange("p a c r -> p a r c"),
+            )
+            st["qw", u, h] = qw
+
+        def qq(u, h):
+            st["qc", u, h] = quantize(st["qw", u, h][:], "q", 2 * P)
+
+        def wr(b, g):
+            if g == 0:
+                st["d", b] = [psum_d.tile([P, E], F32, name=f"d{j}") for j in range(4)]
+            (kc, ks), (vc, vs) = st["kc", ("k", b, g)], st["vc", b, g]
             for j in range(4):
-                nc.scalar.activation(out=s0g[:, j, :], in_=s0r[b][:, j, :], func=ACT.Copy, scale=g07[:, j : j + 1])
+                cols = slice(128 * j, 128 * (j + 1))
+                nc.tensor.matmul_mx(
+                    out=st["d", b][j][:],
+                    lhsT=kc[:, cols].bitcast(X4),
+                    lhsT_scale=ks[:, cols],
+                    rhs=vc[:].bitcast(X4),
+                    rhs_scale=vs[:],
+                    start=(g == 0),
+                    stop=(g == G - 1),
+                )
+
+        def sp(b):
+            u = work.tile([P, 4, E], F32, name="u")
             for j in range(4):
                 nc.vector.scalar_tensor_tensor(
-                    out=sp[:, j, :], in0=d[j][:], scalar=gs32[:, j : j + 1], in1=s0g[:, j, :], op0=ALU.mult, op1=ALU.add
+                    out=u[:, j, :], in0=s0r[b][:, j, :], scalar=0.7 * 32.0, in1=st["d", b][j][:], op0=ALU.mult, op1=ALU.add
                 )
-            si = work.tile([P, E, 4], BF16, align_bytes=64, name="si")
-            interleave(si[:], sp[:])
-            return quantize(si[:].rearrange("p n t -> p (n t)"), "s")
+            st["u", b] = u
+            st["si", b] = work.tile([P, E, 4], BF16, align_bytes=64, name="si")
 
-        def read(b, g, qq, sq):
-            (qc, qs), (sc, ss) = qq, sq
+        def si(b, c):
+            u = st["u", b]
+            cols = slice(128 * c, 128 * (c + 1))
+            tr = psum_t.tile([P, 4, P], F32, name="tr")
+            for j in range(4):
+                nc.tensor.matmul(tr[:, j, :], lhsT=dgs[:, j, :], rhs=u[:, j, cols], start=True, stop=True)
+            st["ts", b, c] = tr
+
+        def se(b, c):
+            cols = slice(128 * c, 128 * (c + 1))
+            nc.scalar.copy(out=st["si", b][:, cols, :], in_=st["ts", b, c][:].rearrange("p j e -> p e j"))
+
+        def sq(b):
+            st["sc", b] = quantize(st["si", b][:].rearrange("p n t -> p (n t)"), "s")
+
+        def qo(u, h, a):
+            (qc, qs), (sc, ss) = st["qc", u, h], st["sc", u[1]]
+            cols = slice(128 * a, 128 * (a + 1))
+            o = psum_o.tile([P, E], F32, name="o")
+            nc.tensor.matmul_mx(
+                out=o[:],
+                lhsT=qc[:, cols].bitcast(X4),
+                lhsT_scale=qs[:, cols],
+                rhs=sc[:].bitcast(X4),
+                rhs_scale=ss[:],
+                start=True,
+                stop=True,
+            )
+            st["o", u, h, a] = o
+
+        def oe(u, h, a):
+            kind, b, g = u
+            if ("ot", u, h) not in st:
+                st["ot", u, h] = outs.tile([P, 2, E], F32, name="ot")
+            ot, o = st["ot", u, h], st["o", u, h, a]
+            if (u, h, a) in EVAC_VECTOR:
+                nc.vector.tensor_scalar(out=ot[:, a, :], in0=o[:], scalar1=512.0**-0.5, scalar2=None, op0=ALU.mult)
+            else:
+                nc.scalar.activation(out=ot[:, a, :], in_=o[:], func=ACT.Copy, scale=512.0**-0.5)
+
+        def od(u, h):
+            kind, b, g = u
             ov = out[b].rearrange("(g p j) e -> g p j e", p=P, j=J)[g]
-            for h in range(2):
-                ot = work.tile([P, 2, E], F32, name="ot")
-                for a in range(2):
-                    cols = slice(128 * (2 * h + a), 128 * (2 * h + a + 1))
-                    o = psum_o.tile([P, E], F32, name="o")
-                    nc.tensor.matmul_mx(
-                        out=o[:],
-                        lhsT=qc[:, cols].bitcast(X4),
-                        lhsT_scale=qs[:, cols],
-                        rhs=sc[:].bitcast(X4),
-                        rhs_scale=ss[:],
-                        start=True,
-                        stop=True,
-                    )
-                    nc.scalar.activation(out=ot[:, a, :], in_=o[:], func=ACT.Copy, scale=512.0**-0.5)
-                nc.sync.dma_start(out=ov[:, 2 * h : 2 * h + 2, :], in_=ot[:])
+            nc.sync.dma_start(out=ov[:, 2 * h : 2 * h + 2, :], in_=st["ot", u, h][:])
 
-        nc.vector.tensor_scalar(out=gq_t[:, A:F], in0=gq_t[:, A:F], scalar1=-1.0, scalar2=None, op0=ALU.mult)
-        for b in range(B):
-            zk = [front(xk[b, g], absb[:, b * G + g, :]) for g in range(G)]
-            vq = []
-            kq = []
-            for g in range(G):
-                vq.append(v_all(b, g))
-                kq.append(k_back(zk[g][0], zk[g][1]))
-            zq = [front(xq[b, g], None) for g in range(G)]
-            d = write(b, [(kq[g], vq[g]) for g in range(G)])
-            sq = state(b, d)
-            qm = [q_mid(zq[g][0], zq[g][1]) for g in range(G)]
-            for g in range(G):
-                read(b, g, qm[g], sq)
+        def K(b, g):
+            return ("k", b, g)
+
+        def Q(b, g):
+            return ("q", b, g)
+
+        with tc.manual_schedule():
+            xn(K(0, 0))
+            vw(0, 0)
+            xw(K(0, 0))
+            xz(K(0, 0))
+            xn(K(0, 1))
+            xn(K(1, 0))
+            xw(K(0, 1))
+            vw(0, 1)
+            vi(0, 0)
+            xz(K(0, 1))
+            xw(K(1, 0))
+            xs(K(0, 0))
+            xs(K(0, 1))
+            vi(0, 1)
+            xr(K(0, 0))
+            xm(K(0, 0))
+            kz(K(0, 0))
+            xz(K(1, 0))
+            xr(K(0, 1))
+            vq(0, 1)
+            vq(0, 0)
+            xm(K(0, 1))
+            kz(K(0, 1))
+            xn(K(1, 1))
+            xw(K(1, 1))
+            xn(Q(0, 1))
+            ki(K(0, 0))
+            xz(K(1, 1))
+            xs(K(1, 0))
+            vw(1, 1)
+            xn(Q(1, 0))
+            xn(Q(0, 0))
+            xn(Q(1, 1))
+            ki(K(0, 1))
+            vw(1, 0)
+            kh(K(0, 0))
+            xr(K(1, 0))
+            kh(K(0, 1))
+            kq(K(0, 0))
+            kq(K(0, 1))
+            vi(1, 1)
+            xs(K(1, 1))
+            wr(0, 0)
+            wr(0, 1)
+            xw(Q(1, 0))
+            sp(0)
+            xr(K(1, 1))
+            xz(Q(1, 0))
+            xm(K(1, 0))
+            xm(K(1, 1))
+            cd()
+            vi(1, 0)
+            xw(Q(0, 0))
+            vq(1, 1)
+            kz(K(1, 0))
+            xs(Q(1, 0))
+            ki(K(1, 0))
+            si(0, 0)
+            se(0, 0)
+            si(0, 3)
+            se(0, 3)
+            xz(Q(0, 0))
+            kh(K(1, 0))
+            xw(Q(0, 1))
+            kz(K(1, 1))
+            ki(K(1, 1))
+            cg()
+            xw(Q(1, 1))
+            xr(Q(1, 0))
+            si(0, 1)
+            kh(K(1, 1))
+            vq(1, 0)
+            xs(Q(0, 0))
+            kq(K(1, 0))
+            qy(Q(1, 0))
+            qg(Q(1, 0), 1)
+            xr(Q(0, 0))
+            qy(Q(0, 0))
+            si(0, 2)
+            se(0, 2)
+            kq(K(1, 1))
+            se(0, 1)
+            xz(Q(1, 1))
+            wr(1, 0)
+            wr(1, 1)
+            qt(Q(1, 0), 1)
+            sp(1)
+            qe(Q(1, 0), 1)
+            qq(Q(1, 0), 1)
+            si(1, 1)
+            xz(Q(0, 1))
+            si(1, 3)
+            qg(Q(0, 0), 0)
+            xs(Q(1, 1))
+            se(1, 1)
+            qg(Q(1, 0), 0)
+            se(1, 3)
+            xs(Q(0, 1))
+            si(1, 0)
+            si(1, 2)
+            xr(Q(1, 1))
+            qg(Q(0, 0), 1)
+            qy(Q(1, 1))
+            se(1, 0)
+            qt(Q(1, 0), 0)
+            se(1, 2)
+            qe(Q(1, 0), 0)
+            sq(1)
+            qt(Q(0, 0), 1)
+            qe(Q(0, 0), 1)
+            qq(Q(1, 0), 0)
+            qo(Q(1, 0), 1, 1)
+            oe(Q(1, 0), 1, 1)
+            xr(Q(0, 1))
+            qo(Q(1, 0), 0, 1)
+            qg(Q(1, 1), 1)
+            qt(Q(0, 0), 0)
+            oe(Q(1, 0), 0, 1)
+            sq(0)
+            qo(Q(1, 0), 0, 0)
+            oe(Q(1, 0), 0, 0)
+            qt(Q(1, 1), 1)
+            qy(Q(0, 1))
+            qq(Q(0, 0), 1)
+            qe(Q(0, 0), 0)
+            qg(Q(0, 1), 0)
+            qo(Q(1, 0), 1, 0)
+            qe(Q(1, 1), 1)
+            oe(Q(1, 0), 1, 0)
+            qo(Q(0, 0), 1, 1)
+            oe(Q(0, 0), 1, 1)
+            qo(Q(0, 0), 1, 0)
+            qq(Q(1, 1), 1)
+            oe(Q(0, 0), 1, 0)
+            qg(Q(0, 1), 1)
+            qt(Q(0, 1), 0)
+            qo(Q(1, 1), 1, 0)
+            qe(Q(0, 1), 0)
+            qq(Q(0, 1), 0)
+            qt(Q(0, 1), 1)
+            qo(Q(0, 1), 0, 0)
+            oe(Q(1, 1), 1, 0)
+            qg(Q(1, 1), 0)
+            qo(Q(0, 1), 0, 1)
+            qe(Q(0, 1), 1)
+            oe(Q(0, 1), 0, 1)
+            qt(Q(1, 1), 0)
+            qo(Q(1, 1), 1, 1)
+            qq(Q(0, 1), 1)
+            od(Q(1, 0), 1)
+            oe(Q(0, 1), 0, 0)
+            qq(Q(0, 0), 0)
+            qe(Q(1, 1), 0)
+            od(Q(0, 0), 1)
+            oe(Q(1, 1), 1, 1)
+            qo(Q(0, 0), 0, 0)
+            qq(Q(1, 1), 0)
+            od(Q(1, 0), 0)
+            oe(Q(0, 0), 0, 0)
+            qo(Q(0, 1), 1, 0)
+            od(Q(0, 1), 0)
+            od(Q(1, 1), 1)
+            qo(Q(0, 1), 1, 1)
+            oe(Q(0, 1), 1, 0)
+            oe(Q(0, 1), 1, 1)
+            od(Q(0, 1), 1)
+            qo(Q(1, 1), 0, 1)
+            qo(Q(1, 1), 0, 0)
+            oe(Q(1, 1), 0, 0)
+            qo(Q(0, 0), 0, 1)
+            oe(Q(1, 1), 0, 1)
+            od(Q(1, 1), 0)
+            oe(Q(0, 0), 0, 1)
+            od(Q(0, 0), 0)

@@ -9,6 +9,8 @@ P = 128
 J = 4
 GT = P * J
 G = T // GT
+X0 = 8
+XW = X0 + A
 
 F32 = mybir.dt.float32
 BF16 = mybir.dt.bfloat16
@@ -18,11 +20,8 @@ F8 = mybir.dt.float8_e4m3fn
 X4 = mybir.dt.float8_e4m3fn_x4
 ALU = mybir.AluOpType
 ACT = mybir.ActivationFunctionType
-I32 = mybir.dt.int32
-SIGNS = -0x7FFF8000
-SHIFT_SCALAR = {("k", 0, 0)}
-Y_VECTOR = {("q", 0, 1), ("q", 1, 1)}
-EVAC_VECTOR = {(("q", 1, 1), 1, 1), (("q", 1, 1), 0, 1)}
+Y_VECTOR = set()
+EVAC_VECTOR = {(1, 1, 1), (1, 1, 3), (1, 0, 1), (1, 0, 3)}
 
 FLOPS = 2 * 2 * B * T * F * E
 
@@ -33,36 +32,25 @@ def tile_dpfpfastweightwriteread_kernel(tc, q, k, v_bytes, v_scale, beta, s0, gq
     with ExitStack() as ctx:
         const = ctx.enter_context(tc.tile_pool(name="const", bufs=1))
         loads = ctx.enter_context(tc.tile_pool(name="loads", bufs=1))
-        work = ctx.enter_context(tc.tile_pool(name="work", bufs=3))
-        outs = ctx.enter_context(tc.tile_pool(name="outs", bufs=5))
-        zpool = ctx.enter_context(tc.tile_pool(name="zpool", bufs=4))
+        work = ctx.enter_context(tc.tile_pool(name="work", bufs=2))
+        small = ctx.enter_context(tc.tile_pool(name="small", bufs=4))
+        outs = ctx.enter_context(tc.tile_pool(name="outs", bufs=8))
+        zpool = ctx.enter_context(tc.tile_pool(name="zpool", bufs=3))
         codes = ctx.enter_context(tc.tile_pool(name="codes", bufs=3))
         psum_d = ctx.enter_context(tc.psum_pool(name="psum_d", bufs=1))
         psum_o = ctx.enter_context(tc.psum_pool(name="psum_o", bufs=2))
         psum_t = ctx.enter_context(tc.psum_pool(name="psum_t", bufs=2))
 
-        x_t, xn_t, vb, s0r = {}, {}, {}, {}
+        x_t, vb, s0r = {}, {}, {}
+        for b in range(B):
+            for kind in ("k", "q"):
+                x_t[kind, b] = loads.tile([P, G * J, XW], BF16, name=f"x{kind}{b}")
 
         def load_x(kind, b, g):
             src = k if kind == "k" else q
-            flat = src.rearrange("b t a -> (b t a)")
-            size = GT * A
-            base = (b * G + g) * size
-            row = J * A
-            x = loads.tile([P, J, A], BF16, name=f"x{kind}{b}{g}")
-            nc.sync.dma_start(out=x[:], in_=src[b].rearrange("(g p j) a -> g p j a", p=P, j=J)[g])
-            xn = loads.tile([P, J, A], BF16, name=f"xn{kind}{b}{g}")
-            xnf = xn[:].rearrange("p j a -> p (j a)")
-            if (kind, b, g) in SHIFT_SCALAR:
-                nc.scalar.copy(out=xnf[:, 0 : row - 1], in_=x[:].rearrange("p j a -> p (j a)")[:, 1:row])
-            elif base + size < B * T * A:
-                nc.sync.dma_start(out=xnf, in_=flat[base + 1 : base + 1 + size].rearrange("(p f) -> p f", f=row))
-            else:
-                cut = base + 1 + (P - 1) * row
-                nc.sync.dma_start(out=xnf[0 : P - 1], in_=flat[base + 1 : cut].rearrange("(p f) -> p f", f=row))
-                nc.sync.dma_start(out=xnf[P - 1 : P, 0 : row - 1], in_=flat[cut : base + size].unsqueeze(0))
-            x_t[kind, b, g] = x
-            xn_t[kind, b, g] = xn
+            nc.sync.dma_start(
+                out=x_t[kind, b][:, g * J : (g + 1) * J, X0:XW], in_=src[b].rearrange("(g p j) a -> g p j a", p=P, j=J)[g]
+            )
 
         def load_v(b, g):
             t = loads.tile([P, J, E], U8, name=f"vb{b}{g}")
@@ -87,11 +75,12 @@ def tile_dpfpfastweightwriteread_kernel(tc, q, k, v_bytes, v_scale, beta, s0, gq
                 load_x("k", b, g)
                 load_v(b, g)
             load_s0(b)
-        for b in range(B):
-            for g in range(G):
-                load_x("q", b, g)
-                if b + g == 0:
-                    nc.sync.dma_start(out=gq_t[:], in_=gq.partition_broadcast(P))
+            if b == 0:
+                for g in range(G):
+                    load_x("q", 0, g)
+        for g in range(G):
+            load_x("q", 1, g)
+        nc.sync.dma_start(out=gq_t[:], in_=gq.partition_broadcast(P))
 
         ident = const.tile([P, P], F32, name="ident")
         make_identity(nc, ident[:])
@@ -99,12 +88,17 @@ def tile_dpfpfastweightwriteread_kernel(tc, q, k, v_bytes, v_scale, beta, s0, gq
         one = const.tile([P, 1], F32, name="one")
         nc.vector.memset(one[:], 1.0)
         eps = const.tile([P, 1], F32, name="eps")
-        nc.vector.tensor_scalar(out=eps[:], in0=one[:], scalar1=1e-6, scalar2=None, op0=ALU.mult)
+        nc.vector.tensor_scalar(out=eps[:], in0=one[:], scalar1=2.5e-7, scalar2=None, op0=ALU.mult)
         absb = const.tile([P, B * G, J], F32, name="absb")
         nc.vector.scalar_tensor_tensor(out=absb[:], in0=beta_r[:], scalar=-1.0, in1=beta_r[:], op0=ALU.mult, op1=ALU.max)
         sgn = const.tile([P, B, G * J], F32, name="sgn")
         nc.vector.tensor_scalar(
-            out=sgn[:].rearrange("p b (g j) -> p (b g) j", j=J), in0=beta_r[:], scalar1=0.0, scalar2=0.5, op0=ALU.is_ge, op1=ALU.subtract
+            out=sgn[:].rearrange("p b (g j) -> p (b g) j", j=J),
+            in0=beta_r[:],
+            scalar1=0.0,
+            scalar2=0.5,
+            op0=ALU.is_ge,
+            op1=ALU.subtract,
         )
         vss = const.tile([P, B, G * J], F32, name="vss")
         nc.vector.scalar_tensor_tensor(
@@ -130,60 +124,75 @@ def tile_dpfpfastweightwriteread_kernel(tc, q, k, v_bytes, v_scale, beta, s0, gq
         def cg():
             nc.gpsimd.tensor_scalar(out=gqn[:], in0=gq_t[:, A:F], scalar1=-1.0, scalar2=0.0, op0=ALU.mult, op1=ALU.add)
 
-        def xn(u):
+        def xn(kind, b, g):
+            x = x_t[kind, b][:, g * J : (g + 1) * J, :]
             nc.gpsimd.tensor_scalar(
-                out=xn_t[u][:, :, A - 1 : A], in0=x_t[u][:, :, 0:1], scalar1=-1.0, scalar2=None, op0=ALU.mult
+                out=x[:, :, X0 - 1 : X0], in0=x[:, :, XW - 1 : XW], scalar1=-1.0, scalar2=0.0, op0=ALU.mult, op1=ALU.add
             )
 
-        def xw(u):
-            x, xs_ = x_t[u], xn_t[u]
-            w = work.tile([P, J, A], BF16, name="w")
-            nc.vector.scalar_tensor_tensor(
-                out=w[:].rearrange("p j a -> p (j a)").bitcast(I32),
-                in0=xs_[:].rearrange("p j a -> p (j a)").bitcast(I32),
-                scalar=SIGNS,
-                in1=x[:].rearrange("p j a -> p (j a)").bitcast(I32),
-                op0=ALU.bitwise_and,
-                op1=ALU.bitwise_xor,
+        def xh(kind, b, g, n):
+            h = work.tile([P, n * J, A], BF16, name="h")
+            nc.vector.tensor_scalar(
+                out=h[:],
+                in0=x_t[kind, b][:, g * J : (g + n) * J, X0:XW],
+                scalar1=0.0,
+                scalar2=0.5,
+                op0=ALU.is_ge,
+                op1=ALU.subtract,
             )
-            st["w", u] = w
+            st["h", kind, b, g] = h
 
-        def xz(u):
-            x, w = x_t[u], st["w", u]
-            z = zpool.tile([P, J, A], F32, name="z")
-            nc.vector.scalar_tensor_tensor(
-                out=z[:, :, 1:A], in0=w[:, :, 0 : A - 1], scalar=0.0, in1=x[:, :, 1:A], op0=ALU.max, op1=ALU.mult
+        def xw(kind, b, g, n):
+            w = work.tile([P, n * J, A], BF16, name="w")
+            nc.vector.tensor_tensor(
+                out=w[:], in0=st["h", kind, b, g][:], in1=x_t[kind, b][:, g * J : (g + n) * J, X0 - 1 : XW - 1], op=ALU.mult
             )
-            nc.vector.scalar_tensor_tensor(
-                out=z[:, :, 0:1], in0=w[:, :, A - 1 : A], scalar=0.0, in1=x[:, :, 0:1], op0=ALU.max, op1=ALU.mult
-            )
-            st["z", u] = z
+            st["w", kind, b, g] = w
 
-        def xs(u):
-            z = st["z", u]
-            ss = work.tile([P, J], F32, name="ss")
-            for t in range(J):
-                junk = work.tile([P, A], BF16, name="junk")
+        def xz(kind, b, g, n):
+            if ("z", kind, b) not in st:
+                st["z", kind, b] = zpool.tile([P, G * J, A], F32, name="z")
+                st["ss", kind, b] = small.tile([P, G * J], F32, name="ss")
+                st["rt", kind, b] = small.tile([P, G * J], F32, name="rt")
+                st["inv", kind, b] = small.tile([P, G * J], F32, name="inv")
+            rows = slice(g * J, (g + n) * J)
+            nc.vector.scalar_tensor_tensor(
+                out=st["z", kind, b][:, rows, :],
+                in0=st["w", kind, b, g][:],
+                scalar=0.0,
+                in1=x_t[kind, b][:, rows, X0:XW],
+                op0=ALU.max,
+                op1=ALU.mult,
+            )
+
+        def xs(kind, b, g):
+            z, ss = st["z", kind, b], st["ss", kind, b]
+            for t in range(g * J, (g + 1) * J):
+                junk = small.tile([P, A], BF16, name="junk")
                 nc.scalar.activation(out=junk[:], in_=z[:, t, :], func=ACT.Square, accum_out=ss[:, t : t + 1])
-            rt = work.tile([P, J], F32, name="rt")
-            nc.scalar.activation(out=rt[:], in_=ss[:], func=ACT.Sqrt, scale=1.0 / 512.0, bias=eps[:])
-            st["rt", u] = rt
 
-        def xr(u):
-            kind, b, g = u
-            inv = zpool.tile([P, J], F32, name="inv")
-            nc.vector.reciprocal(out=inv[:], in_=st["rt", u][:])
-            st["inv", u] = inv
+        def xr(kind, b, g, n):
+            cols = slice(g * J, (g + n) * J)
+            nc.scalar.activation(
+                out=st["inv", kind, b][:, cols],
+                in_=st["ss", kind, b][:, cols],
+                func=ACT.Abs_reciprocal_sqrt,
+                scale=1.0 / 512.0,
+                bias=eps[:],
+            )
 
-        def xm(u):
-            kind, b, g = u
-            if kind == "k":
-                inv = st["inv", u]
-                sk = zpool.tile([P, J], F32, name="sk")
-                nc.gpsimd.tensor_tensor(out=sk[:], in0=inv[:], in1=absb[:, b * G + g, :], op=ALU.mult)
-                st["inv", u] = sk
+        def xm(b, g, n):
+            sk = small.tile([P, n * J], F32, name="sk")
+            nc.gpsimd.tensor_tensor(
+                out=sk[:],
+                in0=st["inv", "k", b][:, g * J : (g + n) * J],
+                in1=absb[:, b * G + g : b * G + g + n, :].rearrange("p n j -> p (n j)"),
+                op=ALU.mult,
+            )
+            for m in range(n):
+                st["sk", b, g + m] = sk[:, m * J : (m + 1) * J]
 
-        def quantize(src, name, width=GT):
+        def quantize(src, name, width):
             c = codes.tile([P, width], U32, align_bytes=64, name=name + "c")
             s = codes.tile([P, width], U8, align_bytes=64, name=name + "s")
             nc.vector.quantize_mx(out=c[:].bitcast(X4), scales=s[:], in_=src)
@@ -194,33 +203,59 @@ def tile_dpfpfastweightwriteread_kernel(tc, q, k, v_bytes, v_scale, beta, s0, gq
                 out=dst.rearrange("p (c i) t -> p c t i", i=4), in_=src.rearrange("p t (c i) -> p c t i", i=4)
             )
 
-        def kz(u):
-            z, sk = st["z", u], st["inv", u]
+        def kz(b, g):
+            z, sk = st["z", "k", b], st["sk", b, g]
             zs = work.tile([P, J, A], BF16, name="zs")
             for t in range(J):
                 nc.scalar.activation(
                     out=zs[:, t, :].rearrange("p (j m) -> p j m", j=4),
-                    in_=z[:, t, :].rearrange("p (m j) -> p j m", j=4),
+                    in_=z[:, g * J + t, :].rearrange("p (m j) -> p j m", j=4),
                     func=ACT.Copy,
                     scale=sk[:, t : t + 1],
                 )
-            st["zs", u] = zs
+            st["zs", b, g] = zs
 
-        def ki(u):
+        def ki(b, g):
             zi = work.tile([P, A, J], BF16, name="zi")
-            interleave(zi[:], st["zs", u][:])
-            st["zi", u] = zi
+            interleave(zi[:], st["zs", b, g][:])
+            st["zi", b, g] = zi
 
-        def kh(u):
+        def kd(b, g):
+            dg = work.tile([P, J, P], F32, name="dg")
+            for t in range(J):
+                nc.scalar.activation(out=dg[:, t, :], in_=ident[:], func=ACT.Copy, scale=st["sk", b, g][:, t : t + 1])
+            st["dg", b, g] = dg
+
+        def kp(b, g, c):
+            tr = psum_t.tile([P, J, P], F32, name="tr")
+            for t in range(J):
+                nc.tensor.matmul(
+                    tr[:, t, :],
+                    lhsT=st["dg", b, g][:, t, :],
+                    rhs=st["z", "k", b][:, g * J + t, c * P : (c + 1) * P],
+                    start=True,
+                    stop=True,
+                )
+            st["kp", b, g, c] = tr
+
+        def ke(b, g, c):
+            if ("zi", b, g) not in st:
+                st["zi", b, g] = work.tile([P, A, J], BF16, name="zi")
+            nc.scalar.copy(
+                out=st["zi", b, g][:].rearrange("p (j m) t -> p j m t", j=4)[:, :, 32 * c : 32 * (c + 1), :],
+                in_=st["kp", b, g, c][:].rearrange("p t (m j) -> p j m t", j=4),
+            )
+
+        def kh(b, g):
             kw = work.tile([P, F, J], BF16, align_bytes=64, name="kw")
             kwv = kw[:].rearrange("p (j h m) t -> p h j (m t)", j=4, h=2)
-            ziv = st["zi", u][:].rearrange("p (j m) t -> p j (m t)", j=4)
+            ziv = st["zi", b, g][:].rearrange("p (j m) t -> p j (m t)", j=4)
             nc.vector.tensor_scalar(out=kwv[:, 0], in0=ziv, scalar1=0.0, scalar2=None, op0=ALU.max)
             nc.vector.tensor_scalar(out=kwv[:, 1], in0=ziv, scalar1=-1.0, scalar2=0.0, op0=ALU.mult, op1=ALU.max)
-            st["kw", u] = kw
+            st["kw", b, g] = kw
 
-        def kq(u):
-            st["kc", u] = quantize(st["kw", u][:].rearrange("p n t -> p (n t)"), "kw")
+        def kq(b, g):
+            st["kc", b, g] = quantize(st["kw", b, g][:].rearrange("p n t -> p (n t)"), "kw", GT)
 
         def vw(b, g):
             t_ = work.tile([P, J, E], BF16, name="vw")
@@ -239,58 +274,12 @@ def tile_dpfpfastweightwriteread_kernel(tc, q, k, v_bytes, v_scale, beta, s0, gq
             st["vi", b, g] = t_
 
         def vq(b, g):
-            st["vc", b, g] = quantize(st["vi", b, g][:].rearrange("p n t -> p (n t)"), "v")
-
-        def qy(u):
-            y = work.tile([P, J, A], F32, name="y")
-            for t in range(J):
-                if u in Y_VECTOR:
-                    nc.vector.tensor_scalar(
-                        out=y[:, t, :], in0=st["z", u][:, t, :], scalar1=st["inv", u][:, t : t + 1], scalar2=None, op0=ALU.mult
-                    )
-                else:
-                    nc.scalar.activation(out=y[:, t, :], in_=st["z", u][:, t, :], func=ACT.Copy, scale=st["inv", u][:, t : t + 1])
-            st["y", u] = y
-
-        def qg(u, hh):
-            y = st["y", u]
-            qf = work.tile([P, 2, F], BF16, name="qf")
-            t0, t1 = 2 * hh, 2 * hh + 2
-            st["qf", u, hh] = qf
-            for h, op, gain in ((0, ALU.max, gq_t[:, 0:A]), (1, ALU.min, gqn[:])):
-                nc.vector.scalar_tensor_tensor(
-                    out=qf[:, :, h * A : (h + 1) * A],
-                    in0=y[:, t0:t1, :],
-                    scalar=0.0,
-                    in1=gain.unsqueeze(1).to_broadcast([P, t1 - t0, A]),
-                    op0=op,
-                    op1=ALU.mult,
-                )
-
-        def qt(u, h):
-            words = st["qf", u, h][:].bitcast(F32)
-            tr = psum_t.tile([P, 2, 2, P], F32, name="tr")
-            for a in range(2):
-                for c in range(2):
-                    nc.tensor.transpose(tr[:, a, c, :], words[:, a, c : F // 2 : 2], ident[:])
-            st["tr", u, h] = tr
-
-        def qe(u, h):
-            tr = st["tr", u, h]
-            qw = work.tile([P, 2 * P * 4], BF16, align_bytes=64, name="qw")
-            nc.scalar.copy(
-                out=qw[:].bitcast(F32).rearrange("p (a r c) -> p a r c", a=2, c=2),
-                in_=tr[:].rearrange("p a c r -> p a r c"),
-            )
-            st["qw", u, h] = qw
-
-        def qq(u, h):
-            st["qc", u, h] = quantize(st["qw", u, h][:], "q", 2 * P)
+            st["vc", b, g] = quantize(st["vi", b, g][:].rearrange("p n t -> p (n t)"), "v", GT)
 
         def wr(b, g):
             if g == 0:
                 st["d", b] = [psum_d.tile([P, E], F32, name=f"d{j}") for j in range(4)]
-            (kc, ks), (vc, vs) = st["kc", ("k", b, g)], st["vc", b, g]
+            (kc, ks), (vc, vs) = st["kc", b, g], st["vc", b, g]
             for j in range(4):
                 cols = slice(128 * j, 128 * (j + 1))
                 nc.tensor.matmul_mx(
@@ -313,228 +302,273 @@ def tile_dpfpfastweightwriteread_kernel(tc, q, k, v_bytes, v_scale, beta, s0, gq
             st["si", b] = work.tile([P, E, 4], BF16, align_bytes=64, name="si")
 
         def si(b, c):
-            u = st["u", b]
-            cols = slice(128 * c, 128 * (c + 1))
-            tr = psum_t.tile([P, 4, P], F32, name="tr")
+            tr = psum_d.tile([P, 4, P], F32, name=f"d{c}")
             for j in range(4):
-                nc.tensor.matmul(tr[:, j, :], lhsT=dgs[:, j, :], rhs=u[:, j, cols], start=True, stop=True)
+                nc.tensor.matmul(
+                    tr[:, j, :], lhsT=dgs[:, j, :], rhs=st["u", b][:, j, c * P : (c + 1) * P], start=True, stop=True
+                )
             st["ts", b, c] = tr
 
         def se(b, c):
-            cols = slice(128 * c, 128 * (c + 1))
-            nc.scalar.copy(out=st["si", b][:, cols, :], in_=st["ts", b, c][:].rearrange("p j e -> p e j"))
+            nc.scalar.copy(out=st["si", b][:, c * P : (c + 1) * P, :], in_=st["ts", b, c][:].rearrange("p j e -> p e j"))
 
         def sq(b):
-            st["sc", b] = quantize(st["si", b][:].rearrange("p n t -> p (n t)"), "s")
+            st["sc", b] = quantize(st["si", b][:].rearrange("p n t -> p (n t)"), "s", E)
 
-        def qo(u, h, a):
-            (qc, qs), (sc, ss) = st["qc", u, h], st["sc", u[1]]
-            cols = slice(128 * a, 128 * (a + 1))
-            o = psum_o.tile([P, E], F32, name="o")
+        def qy(b, g):
+            y = work.tile([P, J, A], F32, name="y")
+            for t in range(J):
+                n = g * J + t
+                if (b, g) in Y_VECTOR:
+                    nc.vector.tensor_scalar(
+                        out=y[:, t, :],
+                        in0=st["z", "q", b][:, n, :],
+                        scalar1=st["inv", "q", b][:, n : n + 1],
+                        scalar2=None,
+                        op0=ALU.mult,
+                    )
+                else:
+                    nc.scalar.activation(
+                        out=y[:, t, :], in_=st["z", "q", b][:, n, :], func=ACT.Copy, scale=st["inv", "q", b][:, n : n + 1]
+                    )
+            st["y", b, g] = y
+
+        def qg(b, g, t, n):
+            if ("qf", b, g) not in st:
+                st["qf", b, g] = work.tile([P, J, F], BF16, name="qf")
+            for h, op, gain in ((0, ALU.max, gq_t[:, 0:A]), (1, ALU.min, gqn[:])):
+                nc.vector.scalar_tensor_tensor(
+                    out=st["qf", b, g][:, t : t + n, h * A : (h + 1) * A],
+                    in0=st["y", b, g][:, t : t + n, :],
+                    scalar=0.0,
+                    in1=gain.unsqueeze(1).to_broadcast([P, n, A]),
+                    op0=op,
+                    op1=ALU.mult,
+                )
+
+        def qt(b, g, h):
+            words = st["qf", b, g][:].bitcast(F32)
+            tr = psum_t.tile([P, 2, 2, P], F32, name="tr")
+            for a in range(2):
+                for c in range(2):
+                    nc.tensor.transpose(tr[:, a, c, :], words[:, 2 * h + a, c : F // 2 : 2], ident[:])
+            st["tr", b, g, h] = tr
+
+        def qe(b, g, h):
+            if ("qw", b, g) not in st:
+                st["qw", b, g] = work.tile([P, GT * 4], BF16, align_bytes=64, name="qw")
+            nc.scalar.copy(
+                out=st["qw", b, g][:].bitcast(F32)[:, h * GT : (h + 1) * GT].rearrange("p (a r c) -> p a r c", a=2, c=2),
+                in_=st["tr", b, g, h][:].rearrange("p a c r -> p a r c"),
+            )
+
+        def qq(b, g, t, n):
+            c, s = quantize(st["qw", b, g][:, t * 4 * P : (t + n) * 4 * P], "q", n * P)
+            for m in range(n):
+                cols = slice(m * P, (m + 1) * P)
+                st["qc", b, g, t + m] = (c[:, cols], s[:, cols])
+
+        def qo(b, g, t):
+            (qc, qs), (sc, ss) = st["qc", b, g, t], st["sc", b]
+            o = psum_o.tile([P, E], F32, name="o") if b == 0 else psum_d.tile([P, E], F32, name=f"d{t}")
             nc.tensor.matmul_mx(
                 out=o[:],
-                lhsT=qc[:, cols].bitcast(X4),
-                lhsT_scale=qs[:, cols],
+                lhsT=qc.bitcast(X4),
+                lhsT_scale=qs,
                 rhs=sc[:].bitcast(X4),
                 rhs_scale=ss[:],
                 start=True,
                 stop=True,
             )
-            st["o", u, h, a] = o
+            st["o", b, g, t] = o
 
-        def oe(u, h, a):
-            kind, b, g = u
-            if ("ot", u, h) not in st:
-                st["ot", u, h] = outs.tile([P, 2, E], F32, name="ot")
-            ot, o = st["ot", u, h], st["o", u, h, a]
-            if (u, h, a) in EVAC_VECTOR:
-                nc.vector.tensor_scalar(out=ot[:, a, :], in0=o[:], scalar1=512.0**-0.5, scalar2=None, op0=ALU.mult)
+        def oe(b, g, t):
+            ot, o = outs.tile([P, E], F32, name="ot"), st["o", b, g, t]
+            st["ot", b, g, t] = ot
+            if (b, g, t) in EVAC_VECTOR:
+                nc.vector.tensor_scalar(out=ot[:], in0=o[:], scalar1=512.0**-0.5, scalar2=None, op0=ALU.mult)
             else:
-                nc.scalar.activation(out=ot[:, a, :], in_=o[:], func=ACT.Copy, scale=512.0**-0.5)
+                nc.scalar.activation(out=ot[:], in_=o[:], func=ACT.Copy, scale=512.0**-0.5)
 
-        def od(u, h):
-            kind, b, g = u
+        def od(b, g, t):
             ov = out[b].rearrange("(g p j) e -> g p j e", p=P, j=J)[g]
-            nc.sync.dma_start(out=ov[:, 2 * h : 2 * h + 2, :], in_=st["ot", u, h][:])
-
-        def K(b, g):
-            return ("k", b, g)
-
-        def Q(b, g):
-            return ("q", b, g)
+            nc.sync.dma_start(out=ov[:, t, :], in_=st["ot", b, g, t][:])
 
         with tc.manual_schedule():
-            xn(K(0, 0))
+            xh("k", 0, 0, 1)
+            xn("k", 0, 0)
+            xw("k", 0, 0, 1)
             vw(0, 0)
-            xw(K(0, 0))
-            xz(K(0, 0))
-            xn(K(0, 1))
-            xn(K(1, 0))
-            xw(K(0, 1))
+            xn("k", 0, 1)
+            xh("k", 0, 1, 1)
+            cd()
+            xz("k", 0, 0, 1)
+            xw("k", 0, 1, 1)
             vw(0, 1)
             vi(0, 0)
-            xz(K(0, 1))
-            xw(K(1, 0))
-            xs(K(0, 0))
-            xs(K(0, 1))
-            vi(0, 1)
-            xr(K(0, 0))
-            xm(K(0, 0))
-            kz(K(0, 0))
-            xz(K(1, 0))
-            xr(K(0, 1))
-            vq(0, 1)
+            xh("q", 0, 0, 2)
             vq(0, 0)
-            xm(K(0, 1))
-            kz(K(0, 1))
-            xn(K(1, 1))
-            xw(K(1, 1))
-            xn(Q(0, 1))
-            ki(K(0, 0))
-            xz(K(1, 1))
-            xs(K(1, 0))
-            vw(1, 1)
-            xn(Q(1, 0))
-            xn(Q(0, 0))
-            xn(Q(1, 1))
-            ki(K(0, 1))
+            xs("k", 0, 0)
+            xn("q", 0, 1)
+            xn("q", 0, 0)
+            xz("k", 0, 1, 1)
             vw(1, 0)
-            kh(K(0, 0))
-            xr(K(1, 0))
-            kh(K(0, 1))
-            kq(K(0, 0))
-            kq(K(0, 1))
-            vi(1, 1)
-            xs(K(1, 1))
-            wr(0, 0)
-            wr(0, 1)
-            xw(Q(1, 0))
-            sp(0)
-            xr(K(1, 1))
-            xz(Q(1, 0))
-            xm(K(1, 0))
-            xm(K(1, 1))
-            cd()
-            vi(1, 0)
-            xw(Q(0, 0))
-            vq(1, 1)
-            kz(K(1, 0))
-            xs(Q(1, 0))
-            ki(K(1, 0))
-            si(0, 0)
-            se(0, 0)
-            si(0, 3)
-            se(0, 3)
-            xz(Q(0, 0))
-            kh(K(1, 0))
-            xw(Q(0, 1))
-            kz(K(1, 1))
-            ki(K(1, 1))
+            xh("k", 1, 0, 2)
+            xw("q", 0, 0, 2)
+            xn("k", 1, 0)
+            xn("k", 1, 1)
+            xw("k", 1, 0, 2)
+            xn("q", 1, 1)
+            xs("k", 0, 1)
             cg()
-            xw(Q(1, 1))
-            xr(Q(1, 0))
-            si(0, 1)
-            kh(K(1, 1))
+            xh("q", 1, 0, 2)
+            xz("k", 1, 0, 2)
+            xn("q", 1, 0)
+            xr("k", 0, 0, 1)
+            xr("k", 0, 1, 1)
+            xm(0, 0, 1)
+            xm(0, 1, 1)
+            kz(0, 0)
+            xz("q", 0, 0, 2)
+            kz(0, 1)
+            xs("k", 1, 1)
+            ki(0, 0)
+            xs("k", 1, 0)
+            ki(0, 1)
+            kh(0, 0)
+            kh(0, 1)
+            xs("q", 0, 1)
+            kq(0, 0)
+            vi(0, 1)
+            wr(0, 0)
+            xr("k", 1, 0, 2)
+            xs("q", 0, 0)
+            xm(1, 0, 2)
+            vi(1, 0)
+            kd(1, 1)
+            kp(1, 1, 1)
+            vw(1, 1)
+            vq(0, 1)
             vq(1, 0)
-            xs(Q(0, 0))
-            kq(K(1, 0))
-            qy(Q(1, 0))
-            qg(Q(1, 0), 1)
-            xr(Q(0, 0))
-            qy(Q(0, 0))
-            si(0, 2)
-            se(0, 2)
-            kq(K(1, 1))
+            kp(1, 1, 0)
+            xw("q", 1, 0, 2)
+            ke(1, 1, 0)
+            kq(0, 1)
+            xr("q", 0, 0, 2)
+            ke(1, 1, 1)
+            xz("q", 1, 0, 2)
+            wr(0, 1)
+            kd(1, 0)
+            qy(0, 0)
+            kp(1, 0, 1)
+            sp(0)
+            kp(1, 0, 0)
+            xs("q", 1, 0)
+            si(0, 1)
+            ke(1, 0, 1)
+            kh(1, 1)
+            ke(1, 0, 0)
+            si(0, 3)
+            qg(0, 0, 0, 4)
             se(0, 1)
-            xz(Q(1, 1))
+            xs("q", 1, 1)
+            si(0, 0)
+            si(0, 2)
+            se(0, 3)
+            kh(1, 0)
+            se(0, 0)
+            kq(1, 1)
+            qt(0, 0, 1)
+            xr("q", 1, 0, 2)
+            se(0, 2)
+            kq(1, 0)
+            qt(0, 0, 0)
+            qe(0, 0, 1)
+            vi(1, 1)
             wr(1, 0)
-            wr(1, 1)
-            qt(Q(1, 0), 1)
-            sp(1)
-            qe(Q(1, 0), 1)
-            qq(Q(1, 0), 1)
-            si(1, 1)
-            xz(Q(0, 1))
-            si(1, 3)
-            qg(Q(0, 0), 0)
-            xs(Q(1, 1))
-            se(1, 1)
-            qg(Q(1, 0), 0)
-            se(1, 3)
-            xs(Q(0, 1))
-            si(1, 0)
-            si(1, 2)
-            xr(Q(1, 1))
-            qg(Q(0, 0), 1)
-            qy(Q(1, 1))
-            se(1, 0)
-            qt(Q(1, 0), 0)
-            se(1, 2)
-            qe(Q(1, 0), 0)
-            sq(1)
-            qt(Q(0, 0), 1)
-            qe(Q(0, 0), 1)
-            qq(Q(1, 0), 0)
-            qo(Q(1, 0), 1, 1)
-            oe(Q(1, 0), 1, 1)
-            xr(Q(0, 1))
-            qo(Q(1, 0), 0, 1)
-            qg(Q(1, 1), 1)
-            qt(Q(0, 0), 0)
-            oe(Q(1, 0), 0, 1)
+            qe(0, 0, 0)
+            qy(0, 1)
             sq(0)
-            qo(Q(1, 0), 0, 0)
-            oe(Q(1, 0), 0, 0)
-            qt(Q(1, 1), 1)
-            qy(Q(0, 1))
-            qq(Q(0, 0), 1)
-            qe(Q(0, 0), 0)
-            qg(Q(0, 1), 0)
-            qo(Q(1, 0), 1, 0)
-            qe(Q(1, 1), 1)
-            oe(Q(1, 0), 1, 0)
-            qo(Q(0, 0), 1, 1)
-            oe(Q(0, 0), 1, 1)
-            qo(Q(0, 0), 1, 0)
-            qq(Q(1, 1), 1)
-            oe(Q(0, 0), 1, 0)
-            qg(Q(0, 1), 1)
-            qt(Q(0, 1), 0)
-            qo(Q(1, 1), 1, 0)
-            qe(Q(0, 1), 0)
-            qq(Q(0, 1), 0)
-            qt(Q(0, 1), 1)
-            qo(Q(0, 1), 0, 0)
-            oe(Q(1, 1), 1, 0)
-            qg(Q(1, 1), 0)
-            qo(Q(0, 1), 0, 1)
-            qe(Q(0, 1), 1)
-            oe(Q(0, 1), 0, 1)
-            qt(Q(1, 1), 0)
-            qo(Q(1, 1), 1, 1)
-            qq(Q(0, 1), 1)
-            od(Q(1, 0), 1)
-            oe(Q(0, 1), 0, 0)
-            qq(Q(0, 0), 0)
-            qe(Q(1, 1), 0)
-            od(Q(0, 0), 1)
-            oe(Q(1, 1), 1, 1)
-            qo(Q(0, 0), 0, 0)
-            qq(Q(1, 1), 0)
-            od(Q(1, 0), 0)
-            oe(Q(0, 0), 0, 0)
-            qo(Q(0, 1), 1, 0)
-            od(Q(0, 1), 0)
-            od(Q(1, 1), 1)
-            qo(Q(0, 1), 1, 1)
-            oe(Q(0, 1), 1, 0)
-            oe(Q(0, 1), 1, 1)
-            od(Q(0, 1), 1)
-            qo(Q(1, 1), 0, 1)
-            qo(Q(1, 1), 0, 0)
-            oe(Q(1, 1), 0, 0)
-            qo(Q(0, 0), 0, 1)
-            oe(Q(1, 1), 0, 1)
-            od(Q(1, 1), 0)
-            oe(Q(0, 0), 0, 1)
-            od(Q(0, 0), 0)
+            qq(0, 0, 0, 4)
+            qy(1, 0)
+            vq(1, 1)
+            qo(0, 0, 0)
+            qo(0, 0, 2)
+            qg(0, 1, 0, 4)
+            wr(1, 1)
+            oe(0, 0, 0)
+            oe(0, 0, 2)
+            od(0, 0, 0)
+            qo(0, 0, 1)
+            qo(0, 0, 3)
+            oe(0, 0, 1)
+            od(0, 0, 2)
+            sp(1)
+            oe(0, 0, 3)
+            qt(0, 1, 1)
+            od(0, 0, 1)
+            qy(1, 1)
+            qt(0, 1, 0)
+            od(0, 0, 3)
+            si(1, 0)
+            qe(0, 1, 1)
+            qg(1, 1, 2, 2)
+            qe(0, 1, 0)
+            si(1, 3)
+            se(1, 0)
+            qq(0, 1, 0, 4)
+            si(1, 1)
+            se(1, 3)
+            qg(1, 1, 0, 2)
+            qo(0, 1, 3)
+            se(1, 1)
+            qg(1, 0, 0, 4)
+            qo(0, 1, 2)
+            qt(1, 1, 0)
+            oe(0, 1, 2)
+            si(1, 2)
+            qe(1, 1, 0)
+            od(0, 1, 2)
+            oe(0, 1, 3)
+            qt(1, 1, 1)
+            se(1, 2)
+            qq(1, 1, 0, 2)
+            od(0, 1, 3)
+            qo(0, 1, 0)
+            qt(1, 0, 1)
+            qe(1, 1, 1)
+            sq(1)
+            qo(0, 1, 1)
+            qe(1, 0, 1)
+            qt(1, 0, 0)
+            qq(1, 1, 2, 2)
+            oe(0, 1, 0)
+            qo(1, 1, 0)
+            qo(1, 1, 3)
+            oe(0, 1, 1)
+            qo(1, 1, 1)
+            oe(1, 1, 3)
+            od(0, 1, 0)
+            qo(1, 1, 2)
+            qe(1, 0, 0)
+            oe(1, 1, 1)
+            od(0, 1, 1)
+            od(1, 1, 3)
+            oe(1, 1, 2)
+            qq(1, 0, 0, 4)
+            od(1, 1, 1)
+            oe(1, 1, 0)
+            od(1, 1, 2)
+            qo(1, 0, 1)
+            qo(1, 0, 3)
+            od(1, 1, 0)
+            oe(1, 0, 1)
+            qo(1, 0, 2)
+            qo(1, 0, 0)
+            oe(1, 0, 2)
+            od(1, 0, 1)
+            oe(1, 0, 3)
+            od(1, 0, 2)
+            oe(1, 0, 0)
+            od(1, 0, 3)
+            od(1, 0, 0)

@@ -9,8 +9,6 @@ P = 128
 J = 4
 GT = P * J
 G = T // GT
-X0 = 8
-XW = X0 + A
 
 F32 = mybir.dt.float32
 BF16 = mybir.dt.bfloat16
@@ -21,7 +19,7 @@ X4 = mybir.dt.float8_e4m3fn_x4
 ALU = mybir.AluOpType
 ACT = mybir.ActivationFunctionType
 Y_VECTOR = set()
-EVAC_VECTOR = {(1, 1, 1), (1, 1, 3), (1, 0, 1), (1, 0, 3)}
+EVAC_VECTOR = {(1, 1, 1), (1, 1, 3)}
 
 FLOPS = 2 * 2 * B * T * F * E
 
@@ -44,12 +42,12 @@ def tile_dpfpfastweightwriteread_kernel(tc, q, k, v_bytes, v_scale, beta, s0, gq
         x_t, vb, s0r = {}, {}, {}
         for b in range(B):
             for kind in ("k", "q"):
-                x_t[kind, b] = loads.tile([P, G * J, XW], BF16, name=f"x{kind}{b}")
+                x_t[kind, b] = loads.tile([P, G * J, A], BF16, name=f"x{kind}{b}")
 
         def load_x(kind, b, g):
             src = k if kind == "k" else q
             nc.sync.dma_start(
-                out=x_t[kind, b][:, g * J : (g + 1) * J, X0:XW], in_=src[b].rearrange("(g p j) a -> g p j a", p=P, j=J)[g]
+                out=x_t[kind, b][:, g * J : (g + 1) * J, :], in_=src[b].rearrange("(g p j) a -> g p j a", p=P, j=J)[g]
             )
 
         def load_v(b, g):
@@ -111,30 +109,19 @@ def tile_dpfpfastweightwriteread_kernel(tc, q, k, v_bytes, v_scale, beta, s0, gq
         )
         gs32 = const.tile([P, J], F32, name="gs32")
         nc.vector.tensor_scalar(out=gs32[:], in0=gs_r[:], scalar1=1.0 / 32.0, scalar2=None, op0=ALU.mult)
-        dgs = const.tile([P, J, P], F32, name="dgs")
+        g07 = const.tile([P, J], F32, name="g07")
+        nc.vector.tensor_scalar(out=g07[:], in0=gs_r[:], scalar1=0.7, scalar2=None, op0=ALU.mult)
         gqn = const.tile([P, A], BF16, name="gqn")
         st = {}
 
-        def cd():
-            for j in range(J):
-                nc.gpsimd.tensor_scalar(
-                    out=dgs[:, j, :], in0=ident[:], scalar1=gs32[:, j : j + 1], scalar2=0.0, op0=ALU.mult, op1=ALU.add
-                )
-
         def cg():
             nc.gpsimd.tensor_scalar(out=gqn[:], in0=gq_t[:, A:F], scalar1=-1.0, scalar2=0.0, op0=ALU.mult, op1=ALU.add)
-
-        def xn(kind, b, g):
-            x = x_t[kind, b][:, g * J : (g + 1) * J, :]
-            nc.gpsimd.tensor_scalar(
-                out=x[:, :, X0 - 1 : X0], in0=x[:, :, XW - 1 : XW], scalar1=-1.0, scalar2=0.0, op0=ALU.mult, op1=ALU.add
-            )
 
         def xh(kind, b, g, n):
             h = work.tile([P, n * J, A], BF16, name="h")
             nc.vector.tensor_scalar(
                 out=h[:],
-                in0=x_t[kind, b][:, g * J : (g + n) * J, X0:XW],
+                in0=x_t[kind, b][:, g * J : (g + n) * J, :],
                 scalar1=0.0,
                 scalar2=0.5,
                 op0=ALU.is_ge,
@@ -143,9 +130,11 @@ def tile_dpfpfastweightwriteread_kernel(tc, q, k, v_bytes, v_scale, beta, s0, gq
             st["h", kind, b, g] = h
 
         def xw(kind, b, g, n):
+            h, x = st["h", kind, b, g], x_t[kind, b][:, g * J : (g + n) * J, :]
             w = work.tile([P, n * J, A], BF16, name="w")
-            nc.vector.tensor_tensor(
-                out=w[:], in0=st["h", kind, b, g][:], in1=x_t[kind, b][:, g * J : (g + n) * J, X0 - 1 : XW - 1], op=ALU.mult
+            nc.vector.tensor_tensor(out=w[:, :, 1:A], in0=h[:, :, 1:A], in1=x[:, :, 0 : A - 1], op=ALU.mult)
+            nc.vector.scalar_tensor_tensor(
+                out=w[:, :, 0:1], in0=x[:, :, A - 1 : A], scalar=-1.0, in1=h[:, :, 0:1], op0=ALU.mult, op1=ALU.mult
             )
             st["w", kind, b, g] = w
 
@@ -153,14 +142,13 @@ def tile_dpfpfastweightwriteread_kernel(tc, q, k, v_bytes, v_scale, beta, s0, gq
             if ("z", kind, b) not in st:
                 st["z", kind, b] = zpool.tile([P, G * J, A], F32, name="z")
                 st["ss", kind, b] = small.tile([P, G * J], F32, name="ss")
-                st["rt", kind, b] = small.tile([P, G * J], F32, name="rt")
                 st["inv", kind, b] = small.tile([P, G * J], F32, name="inv")
             rows = slice(g * J, (g + n) * J)
             nc.vector.scalar_tensor_tensor(
                 out=st["z", kind, b][:, rows, :],
                 in0=st["w", kind, b, g][:],
                 scalar=0.0,
-                in1=x_t[kind, b][:, rows, X0:XW],
+                in1=x_t[kind, b][:, rows, :],
                 op0=ALU.max,
                 op1=ALU.mult,
             )
@@ -220,32 +208,6 @@ def tile_dpfpfastweightwriteread_kernel(tc, q, k, v_bytes, v_scale, beta, s0, gq
             interleave(zi[:], st["zs", b, g][:])
             st["zi", b, g] = zi
 
-        def kd(b, g):
-            dg = work.tile([P, J, P], F32, name="dg")
-            for t in range(J):
-                nc.scalar.activation(out=dg[:, t, :], in_=ident[:], func=ACT.Copy, scale=st["sk", b, g][:, t : t + 1])
-            st["dg", b, g] = dg
-
-        def kp(b, g, c):
-            tr = psum_t.tile([P, J, P], F32, name="tr")
-            for t in range(J):
-                nc.tensor.matmul(
-                    tr[:, t, :],
-                    lhsT=st["dg", b, g][:, t, :],
-                    rhs=st["z", "k", b][:, g * J + t, c * P : (c + 1) * P],
-                    start=True,
-                    stop=True,
-                )
-            st["kp", b, g, c] = tr
-
-        def ke(b, g, c):
-            if ("zi", b, g) not in st:
-                st["zi", b, g] = work.tile([P, A, J], BF16, name="zi")
-            nc.scalar.copy(
-                out=st["zi", b, g][:].rearrange("p (j m) t -> p j m t", j=4)[:, :, 32 * c : 32 * (c + 1), :],
-                in_=st["kp", b, g, c][:].rearrange("p t (m j) -> p j m t", j=4),
-            )
-
         def kh(b, g):
             kw = work.tile([P, F, J], BF16, align_bytes=64, name="kw")
             kwv = kw[:].rearrange("p (j h m) t -> p h j (m t)", j=4, h=2)
@@ -292,25 +254,29 @@ def tile_dpfpfastweightwriteread_kernel(tc, q, k, v_bytes, v_scale, beta, s0, gq
                     stop=(g == G - 1),
                 )
 
+        def sg(b):
+            s0g = work.tile([P, 4, E], F32, name="s0g")
+            for j in range(4):
+                nc.scalar.activation(out=s0g[:, j, :], in_=s0r[b][:, j, :], func=ACT.Copy, scale=g07[:, j : j + 1])
+            st["s0g", b] = s0g
+
         def sp(b):
-            u = work.tile([P, 4, E], F32, name="u")
+            t_ = work.tile([P, 4, E], BF16, name="sp")
             for j in range(4):
                 nc.vector.scalar_tensor_tensor(
-                    out=u[:, j, :], in0=s0r[b][:, j, :], scalar=0.7 * 32.0, in1=st["d", b][j][:], op0=ALU.mult, op1=ALU.add
+                    out=t_[:, j, :],
+                    in0=st["d", b][j][:],
+                    scalar=gs32[:, j : j + 1],
+                    in1=st["s0g", b][:, j, :],
+                    op0=ALU.mult,
+                    op1=ALU.add,
                 )
-            st["u", b] = u
-            st["si", b] = work.tile([P, E, 4], BF16, align_bytes=64, name="si")
+            st["sp", b] = t_
 
-        def si(b, c):
-            tr = psum_d.tile([P, 4, P], F32, name=f"d{c}")
-            for j in range(4):
-                nc.tensor.matmul(
-                    tr[:, j, :], lhsT=dgs[:, j, :], rhs=st["u", b][:, j, c * P : (c + 1) * P], start=True, stop=True
-                )
-            st["ts", b, c] = tr
-
-        def se(b, c):
-            nc.scalar.copy(out=st["si", b][:, c * P : (c + 1) * P, :], in_=st["ts", b, c][:].rearrange("p j e -> p e j"))
+        def si(b):
+            t_ = work.tile([P, E, 4], BF16, align_bytes=64, name="si")
+            interleave(t_[:], st["sp", b][:])
+            st["si", b] = t_
 
         def sq(b):
             st["sc", b] = quantize(st["si", b][:].rearrange("p n t -> p (n t)"), "s", E)
@@ -396,179 +362,152 @@ def tile_dpfpfastweightwriteread_kernel(tc, q, k, v_bytes, v_scale, beta, s0, gq
 
         with tc.manual_schedule():
             xh("k", 0, 0, 1)
-            xn("k", 0, 0)
             xw("k", 0, 0, 1)
-            vw(0, 0)
-            xn("k", 0, 1)
             xh("k", 0, 1, 1)
-            cd()
             xz("k", 0, 0, 1)
             xw("k", 0, 1, 1)
-            vw(0, 1)
+            vw(0, 0)
             vi(0, 0)
-            xh("q", 0, 0, 2)
-            vq(0, 0)
             xs("k", 0, 0)
-            xn("q", 0, 1)
-            xn("q", 0, 0)
-            xz("k", 0, 1, 1)
-            vw(1, 0)
-            xh("k", 1, 0, 2)
-            xw("q", 0, 0, 2)
-            xn("k", 1, 0)
-            xn("k", 1, 1)
-            xw("k", 1, 0, 2)
-            xn("q", 1, 1)
-            xs("k", 0, 1)
-            cg()
-            xh("q", 1, 0, 2)
-            xz("k", 1, 0, 2)
-            xn("q", 1, 0)
+            xh("q", 0, 0, 2)
             xr("k", 0, 0, 1)
-            xr("k", 0, 1, 1)
+            xz("k", 0, 1, 1)
+            xw("q", 0, 0, 2)
+            xh("k", 1, 0, 2)
+            vw(1, 0)
             xm(0, 0, 1)
-            xm(0, 1, 1)
+            xs("k", 0, 1)
             kz(0, 0)
+            cg()
+            xr("k", 0, 1, 1)
             xz("q", 0, 0, 2)
-            kz(0, 1)
-            xs("k", 1, 1)
-            ki(0, 0)
-            xs("k", 1, 0)
-            ki(0, 1)
-            kh(0, 0)
-            kh(0, 1)
             xs("q", 0, 1)
-            kq(0, 0)
-            vi(0, 1)
-            wr(0, 0)
-            xr("k", 1, 0, 2)
-            xs("q", 0, 0)
-            xm(1, 0, 2)
             vi(1, 0)
-            kd(1, 1)
-            kp(1, 1, 1)
-            vw(1, 1)
-            vq(0, 1)
-            vq(1, 0)
-            kp(1, 1, 0)
-            xw("q", 1, 0, 2)
-            ke(1, 1, 0)
-            kq(0, 1)
+            xm(0, 1, 1)
+            xw("k", 1, 0, 2)
+            ki(0, 0)
+            xs("q", 0, 0)
             xr("q", 0, 0, 2)
-            ke(1, 1, 1)
-            xz("q", 1, 0, 2)
-            wr(0, 1)
-            kd(1, 0)
-            qy(0, 0)
-            kp(1, 0, 1)
-            sp(0)
-            kp(1, 0, 0)
-            xs("q", 1, 0)
-            si(0, 1)
-            ke(1, 0, 1)
-            kh(1, 1)
-            ke(1, 0, 0)
-            si(0, 3)
-            qg(0, 0, 0, 4)
-            se(0, 1)
-            xs("q", 1, 1)
-            si(0, 0)
-            si(0, 2)
-            se(0, 3)
-            kh(1, 0)
-            se(0, 0)
-            kq(1, 1)
-            qt(0, 0, 1)
-            xr("q", 1, 0, 2)
-            se(0, 2)
-            kq(1, 0)
-            qt(0, 0, 0)
-            qe(0, 0, 1)
-            vi(1, 1)
-            wr(1, 0)
-            qe(0, 0, 0)
+            xh("q", 1, 0, 2)
             qy(0, 1)
+            xz("k", 1, 0, 2)
+            vq(0, 0)
+            xw("q", 1, 0, 2)
+            kz(0, 1)
+            xs("k", 1, 0)
+            vw(0, 1)
+            qy(0, 0)
+            kh(0, 0)
+            xz("q", 1, 0, 2)
+            xs("k", 1, 1)
+            qg(0, 1, 0, 4)
+            ki(0, 1)
+            qg(0, 0, 0, 4)
+            xs("q", 1, 1)
+            kh(0, 1)
+            vi(0, 1)
+            kq(0, 0)
+            qt(0, 1, 0)
+            qt(0, 1, 1)
+            wr(0, 0)
+            qe(0, 1, 0)
+            qt(0, 0, 0)
+            kq(0, 1)
+            vq(0, 1)
+            xr("k", 1, 0, 2)
+            xm(1, 0, 2)
+            qe(0, 1, 1)
+            kz(1, 0)
+            ki(1, 0)
+            wr(0, 1)
+            qq(0, 1, 0, 4)
+            sg(0)
+            xs("q", 1, 0)
+            kz(1, 1)
+            kh(1, 0)
+            sp(0)
+            xr("q", 1, 0, 2)
+            qe(0, 0, 0)
+            qy(1, 1)
+            qt(0, 0, 1)
+            kq(1, 0)
+            qe(0, 0, 1)
+            qy(1, 0)
+            si(0)
+            vq(1, 0)
+            ki(1, 1)
             sq(0)
             qq(0, 0, 0, 4)
-            qy(1, 0)
-            vq(1, 1)
-            qo(0, 0, 0)
-            qo(0, 0, 2)
-            qg(0, 1, 0, 4)
-            wr(1, 1)
-            oe(0, 0, 0)
-            oe(0, 0, 2)
-            od(0, 0, 0)
-            qo(0, 0, 1)
-            qo(0, 0, 3)
-            oe(0, 0, 1)
-            od(0, 0, 2)
-            sp(1)
-            oe(0, 0, 3)
-            qt(0, 1, 1)
-            od(0, 0, 1)
-            qy(1, 1)
-            qt(0, 1, 0)
-            od(0, 0, 3)
-            si(1, 0)
-            qe(0, 1, 1)
-            qg(1, 1, 2, 2)
-            qe(0, 1, 0)
-            si(1, 3)
-            se(1, 0)
-            qq(0, 1, 0, 4)
-            si(1, 1)
-            se(1, 3)
-            qg(1, 1, 0, 2)
-            qo(0, 1, 3)
-            se(1, 1)
-            qg(1, 0, 0, 4)
-            qo(0, 1, 2)
-            qt(1, 1, 0)
-            oe(0, 1, 2)
-            si(1, 2)
-            qe(1, 1, 0)
-            od(0, 1, 2)
-            oe(0, 1, 3)
-            qt(1, 1, 1)
-            se(1, 2)
-            qq(1, 1, 0, 2)
-            od(0, 1, 3)
-            qo(0, 1, 0)
-            qt(1, 0, 1)
-            qe(1, 1, 1)
-            sq(1)
             qo(0, 1, 1)
-            qe(1, 0, 1)
-            qt(1, 0, 0)
-            qq(1, 1, 2, 2)
-            oe(0, 1, 0)
-            qo(1, 1, 0)
-            qo(1, 1, 3)
+            kh(1, 1)
+            qo(0, 1, 2)
+            qg(1, 1, 0, 2)
+            vw(1, 1)
             oe(0, 1, 1)
-            qo(1, 1, 1)
-            oe(1, 1, 3)
-            od(0, 1, 0)
-            qo(1, 1, 2)
-            qe(1, 0, 0)
-            oe(1, 1, 1)
+            qt(1, 1, 0)
+            qg(1, 0, 0, 4)
+            oe(0, 1, 2)
+            qo(0, 0, 1)
+            qo(0, 1, 0)
+            oe(0, 0, 1)
             od(0, 1, 1)
-            od(1, 1, 3)
-            oe(1, 1, 2)
+            od(0, 0, 1)
+            qt(1, 0, 1)
+            qo(0, 0, 0)
+            oe(0, 1, 0)
+            vi(1, 1)
+            od(0, 1, 2)
+            sg(1)
+            kq(1, 1)
+            wr(1, 0)
+            vq(1, 1)
+            qe(1, 0, 1)
+            qg(1, 1, 2, 2)
+            wr(1, 1)
+            sp(1)
+            qe(1, 1, 0)
+            qo(0, 0, 3)
+            oe(0, 0, 0)
+            oe(0, 0, 3)
+            qt(1, 1, 1)
+            qe(1, 1, 1)
+            qq(1, 1, 0, 2)
+            qo(0, 0, 2)
+            od(0, 0, 0)
+            od(0, 0, 3)
+            qo(0, 1, 3)
+            oe(0, 1, 3)
+            si(1)
+            sq(1)
+            od(0, 1, 0)
+            qt(1, 0, 0)
+            oe(0, 0, 2)
+            od(0, 1, 3)
+            qe(1, 0, 0)
+            qq(1, 1, 2, 2)
+            od(0, 0, 2)
+            qo(1, 1, 0)
             qq(1, 0, 0, 4)
-            od(1, 1, 1)
             oe(1, 1, 0)
-            od(1, 1, 2)
-            qo(1, 0, 1)
+            qo(1, 1, 2)
+            qo(1, 1, 1)
             qo(1, 0, 3)
-            od(1, 1, 0)
-            oe(1, 0, 1)
-            qo(1, 0, 2)
             qo(1, 0, 0)
-            oe(1, 0, 2)
-            od(1, 0, 1)
+            od(1, 1, 0)
+            oe(1, 1, 1)
+            qo(1, 0, 1)
+            oe(1, 1, 2)
+            od(1, 1, 2)
             oe(1, 0, 3)
-            od(1, 0, 2)
-            oe(1, 0, 0)
+            od(1, 1, 1)
+            qo(1, 1, 3)
+            qo(1, 0, 2)
+            oe(1, 1, 3)
+            oe(1, 0, 1)
             od(1, 0, 3)
+            od(1, 0, 1)
+            od(1, 1, 3)
+            oe(1, 0, 2)
+            oe(1, 0, 0)
+            od(1, 0, 2)
             od(1, 0, 0)

@@ -9,17 +9,19 @@ P = 128
 J = 4
 GT = P * J
 G = T // GT
+SIGNS = -0x7FFF8000
 
 F32 = mybir.dt.float32
 BF16 = mybir.dt.bfloat16
 U32 = mybir.dt.uint32
+I32 = mybir.dt.int32
 U8 = mybir.dt.uint8
 F8 = mybir.dt.float8_e4m3fn
 X4 = mybir.dt.float8_e4m3fn_x4
 ALU = mybir.AluOpType
 ACT = mybir.ActivationFunctionType
 Y_VECTOR = set()
-EVAC_VECTOR = {(1, 1, 1), (1, 1, 3)}
+EVAC_VECTOR = {(1, 1, 1), (1, 1, 3), (1, 0, 3)}
 
 FLOPS = 2 * 2 * B * T * F * E
 
@@ -39,16 +41,22 @@ def tile_dpfpfastweightwriteread_kernel(tc, q, k, v_bytes, v_scale, beta, s0, gq
         psum_o = ctx.enter_context(tc.psum_pool(name="psum_o", bufs=2))
         psum_t = ctx.enter_context(tc.psum_pool(name="psum_t", bufs=2))
 
-        x_t, vb, s0r = {}, {}, {}
+        x_t, xn_t, vb, s0r = {}, {}, {}, {}
         for b in range(B):
             for kind in ("k", "q"):
                 x_t[kind, b] = loads.tile([P, G * J, A], BF16, name=f"x{kind}{b}")
+                xn_t[kind, b] = loads.tile([P, G * J, A], BF16, name=f"xn{kind}{b}")
 
-        def load_x(kind, b, g):
+        def load_x(kind, b, g, r=0, n=J):
             src = k if kind == "k" else q
-            nc.sync.dma_start(
-                out=x_t[kind, b][:, g * J : (g + 1) * J, :], in_=src[b].rearrange("(g p j) a -> g p j a", p=P, j=J)[g]
-            )
+            rows = src[b].rearrange("(g p j) a -> g p (j a)", p=P, j=J)[g]
+            c0, c1 = r * A, (r + n) * A
+            x = x_t[kind, b][:].rearrange("p t a -> p (t a)")
+            xs_ = xn_t[kind, b][:].rearrange("p t a -> p (t a)")
+            o = g * J * A
+            nc.sync.dma_start(out=x[:, o + c0 : o + c1], in_=rows[:, c0:c1])
+            c2 = min(c1, J * A - 1)
+            nc.sync.dma_start(out=xs_[:, o + c0 : o + c2], in_=rows[:, c0 + 1 : c2 + 1])
 
         def load_v(b, g):
             t = loads.tile([P, J, E], U8, name=f"vb{b}{g}")
@@ -70,8 +78,13 @@ def tile_dpfpfastweightwriteread_kernel(tc, q, k, v_bytes, v_scale, beta, s0, gq
         gq_t = const.tile([P, F], BF16, name="gq_t")
         for b in range(B):
             for g in range(G):
-                load_x("k", b, g)
-                load_v(b, g)
+                if b + g == 0:
+                    load_x("k", 0, 0, 0, 2)
+                    load_v(0, 0)
+                    load_x("k", 0, 0, 2, 2)
+                else:
+                    load_x("k", b, g)
+                    load_v(b, g)
             load_s0(b)
             if b == 0:
                 for g in range(G):
@@ -86,7 +99,9 @@ def tile_dpfpfastweightwriteread_kernel(tc, q, k, v_bytes, v_scale, beta, s0, gq
         one = const.tile([P, 1], F32, name="one")
         nc.vector.memset(one[:], 1.0)
         eps = const.tile([P, 1], F32, name="eps")
-        nc.vector.tensor_scalar(out=eps[:], in0=one[:], scalar1=2.5e-7, scalar2=None, op0=ALU.mult)
+        nc.vector.tensor_scalar(out=eps[:], in0=one[:], scalar1=1e-6, scalar2=None, op0=ALU.mult)
+        warm = const.tile([P, 1], F32, name="warm")
+        nc.scalar.activation(out=warm[:], in_=one[:], func=ACT.Abs_reciprocal_sqrt)
         absb = const.tile([P, B * G, J], F32, name="absb")
         nc.vector.scalar_tensor_tensor(out=absb[:], in0=beta_r[:], scalar=-1.0, in1=beta_r[:], op0=ALU.mult, op1=ALU.max)
         sgn = const.tile([P, B, G * J], F32, name="sgn")
@@ -117,41 +132,38 @@ def tile_dpfpfastweightwriteread_kernel(tc, q, k, v_bytes, v_scale, beta, s0, gq
         def cg():
             nc.gpsimd.tensor_scalar(out=gqn[:], in0=gq_t[:, A:F], scalar1=-1.0, scalar2=0.0, op0=ALU.mult, op1=ALU.add)
 
-        def xh(kind, b, g, n):
-            h = work.tile([P, n * J, A], BF16, name="h")
-            nc.vector.tensor_scalar(
-                out=h[:],
-                in0=x_t[kind, b][:, g * J : (g + n) * J, :],
-                scalar1=0.0,
-                scalar2=0.5,
-                op0=ALU.is_ge,
-                op1=ALU.subtract,
+        def xn(kind, b, r, n):
+            nc.gpsimd.tensor_scalar(
+                out=xn_t[kind, b][:, r : r + n, A - 1 : A],
+                in0=x_t[kind, b][:, r : r + n, 0:1],
+                scalar1=-1.0,
+                scalar2=0.0,
+                op0=ALU.mult,
+                op1=ALU.add,
             )
-            st["h", kind, b, g] = h
 
-        def xw(kind, b, g, n):
-            h, x = st["h", kind, b, g], x_t[kind, b][:, g * J : (g + n) * J, :]
-            w = work.tile([P, n * J, A], BF16, name="w")
-            nc.vector.tensor_tensor(out=w[:, :, 1:A], in0=h[:, :, 1:A], in1=x[:, :, 0 : A - 1], op=ALU.mult)
+        def xw(kind, b, r, n):
+            w = work.tile([P, n, A], BF16, name="w")
             nc.vector.scalar_tensor_tensor(
-                out=w[:, :, 0:1], in0=x[:, :, A - 1 : A], scalar=-1.0, in1=h[:, :, 0:1], op0=ALU.mult, op1=ALU.mult
+                out=w[:].rearrange("p t a -> p (t a)").bitcast(I32),
+                in0=xn_t[kind, b][:, r : r + n, :].rearrange("p t a -> p (t a)").bitcast(I32),
+                scalar=SIGNS,
+                in1=x_t[kind, b][:, r : r + n, :].rearrange("p t a -> p (t a)").bitcast(I32),
+                op0=ALU.bitwise_and,
+                op1=ALU.bitwise_xor,
             )
-            st["w", kind, b, g] = w
+            st["w", kind, b, r] = w
 
-        def xz(kind, b, g, n):
+        def xz(kind, b, r, n):
             if ("z", kind, b) not in st:
                 st["z", kind, b] = zpool.tile([P, G * J, A], F32, name="z")
                 st["ss", kind, b] = small.tile([P, G * J], F32, name="ss")
                 st["inv", kind, b] = small.tile([P, G * J], F32, name="inv")
-            rows = slice(g * J, (g + n) * J)
-            nc.vector.scalar_tensor_tensor(
-                out=st["z", kind, b][:, rows, :],
-                in0=st["w", kind, b, g][:],
-                scalar=0.0,
-                in1=x_t[kind, b][:, rows, :],
-                op0=ALU.max,
-                op1=ALU.mult,
-            )
+            w, x, z = st["w", kind, b, r], x_t[kind, b][:, r : r + n, :], st["z", kind, b][:, r : r + n, :]
+            for dst, src in ((slice(1, A), slice(0, A - 1)), (slice(0, 1), slice(A - 1, A))):
+                nc.vector.scalar_tensor_tensor(
+                    out=z[:, :, dst], in0=w[:, :, src], scalar=0.0, in1=x[:, :, dst], op0=ALU.max, op1=ALU.mult
+                )
 
         def xs(kind, b, g):
             z, ss = st["z", kind, b], st["ss", kind, b]
@@ -361,153 +373,159 @@ def tile_dpfpfastweightwriteread_kernel(tc, q, k, v_bytes, v_scale, beta, s0, gq
             nc.sync.dma_start(out=ov[:, t, :], in_=st["ot", b, g, t][:])
 
         with tc.manual_schedule():
-            xh("k", 0, 0, 1)
-            xw("k", 0, 0, 1)
-            xh("k", 0, 1, 1)
-            xz("k", 0, 0, 1)
-            xw("k", 0, 1, 1)
+            xn("k", 0, 0, 2)
+            xn("k", 0, 2, 2)
+            xn("k", 0, 4, 4)
+            xn("q", 0, 4, 4)
+            xn("q", 0, 0, 4)
+            xw("k", 0, 0, 2)
+            xw("k", 0, 2, 2)
+            xz("k", 0, 0, 2)
+            xz("k", 0, 2, 2)
+            xw("k", 0, 4, 4)
             vw(0, 0)
+            vw(0, 1)
             vi(0, 0)
             xs("k", 0, 0)
-            xh("q", 0, 0, 2)
             xr("k", 0, 0, 1)
-            xz("k", 0, 1, 1)
-            xw("q", 0, 0, 2)
-            xh("k", 1, 0, 2)
-            vw(1, 0)
+            xn("k", 1, 0, 4)
             xm(0, 0, 1)
+            xz("k", 0, 4, 4)
             xs("k", 0, 1)
-            kz(0, 0)
-            cg()
-            xr("k", 0, 1, 1)
-            xz("q", 0, 0, 2)
-            xs("q", 0, 1)
-            vi(1, 0)
-            xm(0, 1, 1)
-            xw("k", 1, 0, 2)
-            ki(0, 0)
-            xs("q", 0, 0)
-            xr("q", 0, 0, 2)
-            xh("q", 1, 0, 2)
-            qy(0, 1)
-            xz("k", 1, 0, 2)
-            vq(0, 0)
-            xw("q", 1, 0, 2)
-            kz(0, 1)
-            xs("k", 1, 0)
-            vw(0, 1)
-            qy(0, 0)
-            kh(0, 0)
-            xz("q", 1, 0, 2)
-            xs("k", 1, 1)
-            qg(0, 1, 0, 4)
-            ki(0, 1)
-            qg(0, 0, 0, 4)
-            xs("q", 1, 1)
-            kh(0, 1)
+            xn("k", 1, 4, 4)
             vi(0, 1)
-            kq(0, 0)
-            qt(0, 1, 0)
-            qt(0, 1, 1)
-            wr(0, 0)
-            qe(0, 1, 0)
-            qt(0, 0, 0)
-            kq(0, 1)
+            kz(0, 0)
+            vq(0, 0)
+            xw("q", 0, 0, 8)
+            xr("k", 0, 1, 1)
+            vw(1, 0)
+            xm(0, 1, 1)
             vq(0, 1)
-            xr("k", 1, 0, 2)
-            xm(1, 0, 2)
-            qe(0, 1, 1)
-            kz(1, 0)
-            ki(1, 0)
+            xw("k", 1, 0, 8)
+            xz("q", 0, 0, 8)
+            ki(0, 0)
+            xn("q", 1, 0, 4)
+            kz(0, 1)
+            xn("q", 1, 4, 4)
+            xs("q", 0, 0)
+            xz("k", 1, 0, 8)
+            xs("q", 0, 1)
+            xs("k", 1, 1)
+            xr("q", 0, 0, 2)
+            xs("k", 1, 0)
+            kh(0, 0)
+            xw("q", 1, 0, 8)
+            kq(0, 0)
+            wr(0, 0)
+            ki(0, 1)
+            xz("q", 1, 0, 8)
+            qy(0, 1)
+            kh(0, 1)
+            vi(1, 0)
+            kq(0, 1)
             wr(0, 1)
-            qq(0, 1, 0, 4)
+            cg()
+            qg(0, 1, 0, 4)
+            qy(0, 0)
             sg(0)
+            xr("k", 1, 0, 2)
+            xs("q", 1, 1)
             xs("q", 1, 0)
-            kz(1, 1)
-            kh(1, 0)
+            xm(1, 0, 2)
             sp(0)
+            kz(1, 0)
+            qt(0, 1, 0)
+            qe(0, 1, 0)
+            qg(0, 0, 0, 4)
             xr("q", 1, 0, 2)
-            qe(0, 0, 0)
+            ki(1, 0)
+            qt(0, 1, 1)
+            qe(0, 1, 1)
             qy(1, 1)
-            qt(0, 0, 1)
-            kq(1, 0)
-            qe(0, 0, 1)
-            qy(1, 0)
+            kz(1, 1)
             si(0)
+            vw(1, 1)
             vq(1, 0)
-            ki(1, 1)
+            qq(0, 1, 0, 4)
+            qt(0, 0, 1)
+            kh(1, 0)
+            qt(0, 0, 0)
+            qe(0, 0, 0)
+            qe(0, 0, 1)
             sq(0)
-            qq(0, 0, 0, 4)
-            qo(0, 1, 1)
-            kh(1, 1)
+            ki(1, 1)
             qo(0, 1, 2)
             qg(1, 1, 0, 2)
-            vw(1, 1)
-            oe(0, 1, 1)
-            qt(1, 1, 0)
-            qg(1, 0, 0, 4)
+            qo(0, 1, 3)
             oe(0, 1, 2)
-            qo(0, 0, 1)
-            qo(0, 1, 0)
-            oe(0, 0, 1)
-            od(0, 1, 1)
-            od(0, 0, 1)
-            qt(1, 0, 1)
-            qo(0, 0, 0)
-            oe(0, 1, 0)
+            kq(1, 0)
+            oe(0, 1, 3)
+            kh(1, 1)
             vi(1, 1)
-            od(0, 1, 2)
-            sg(1)
+            qy(1, 0)
+            qq(0, 0, 0, 4)
             kq(1, 1)
-            wr(1, 0)
+            qt(1, 1, 0)
+            sg(1)
             vq(1, 1)
-            qe(1, 0, 1)
-            qg(1, 1, 2, 2)
-            wr(1, 1)
-            sp(1)
-            qe(1, 1, 0)
+            wr(1, 0)
             qo(0, 0, 3)
-            oe(0, 0, 0)
+            qe(1, 1, 0)
+            qo(0, 1, 0)
+            oe(0, 1, 0)
+            od(0, 1, 0)
+            qg(1, 0, 0, 4)
             oe(0, 0, 3)
+            wr(1, 1)
+            qo(0, 0, 0)
+            oe(0, 0, 0)
+            sp(1)
+            qt(1, 0, 0)
+            qe(1, 0, 0)
+            qo(0, 1, 1)
+            od(0, 1, 3)
+            oe(0, 1, 1)
+            qo(0, 0, 1)
+            qg(1, 1, 2, 2)
+            si(1)
+            qq(1, 1, 0, 2)
+            qt(1, 0, 1)
+            oe(0, 0, 1)
+            qe(1, 0, 1)
+            qo(0, 0, 2)
+            oe(0, 0, 2)
+            od(0, 0, 3)
+            sq(1)
+            od(0, 0, 1)
+            od(0, 0, 0)
             qt(1, 1, 1)
             qe(1, 1, 1)
-            qq(1, 1, 0, 2)
-            qo(0, 0, 2)
-            od(0, 0, 0)
-            od(0, 0, 3)
-            qo(0, 1, 3)
-            oe(0, 1, 3)
-            si(1)
-            sq(1)
-            od(0, 1, 0)
-            qt(1, 0, 0)
-            oe(0, 0, 2)
-            od(0, 1, 3)
-            qe(1, 0, 0)
-            qq(1, 1, 2, 2)
-            od(0, 0, 2)
             qo(1, 1, 0)
+            od(0, 1, 1)
+            qo(1, 1, 1)
             qq(1, 0, 0, 4)
             oe(1, 1, 0)
-            qo(1, 1, 2)
-            qo(1, 1, 1)
-            qo(1, 0, 3)
-            qo(1, 0, 0)
-            od(1, 1, 0)
+            od(0, 1, 2)
+            qq(1, 1, 2, 2)
+            od(0, 0, 2)
             oe(1, 1, 1)
-            qo(1, 0, 1)
-            oe(1, 1, 2)
-            od(1, 1, 2)
-            oe(1, 0, 3)
+            od(1, 1, 0)
+            qo(1, 0, 3)
             od(1, 1, 1)
-            qo(1, 1, 3)
+            oe(1, 0, 3)
             qo(1, 0, 2)
-            oe(1, 1, 3)
-            oe(1, 0, 1)
-            od(1, 0, 3)
-            od(1, 0, 1)
-            od(1, 1, 3)
             oe(1, 0, 2)
+            od(1, 0, 3)
+            qo(1, 0, 0)
+            qo(1, 0, 1)
             oe(1, 0, 0)
+            oe(1, 0, 1)
             od(1, 0, 2)
             od(1, 0, 0)
+            od(1, 0, 1)
+            qo(1, 1, 3)
+            oe(1, 1, 3)
+            qo(1, 1, 2)
+            od(1, 1, 3)
+            oe(1, 1, 2)
+            od(1, 1, 2)

from contextlib import ExitStack

import concourse.mybir as mybir
from concourse.masks import make_identity

B, T, A, E = 2, 1024, 256, 512
F = 2 * A
P = 128
J = 4
GT = P * J
G = T // GT
SIGNS = -0x7FFF8000

F32 = mybir.dt.float32
BF16 = mybir.dt.bfloat16
U32 = mybir.dt.uint32
I32 = mybir.dt.int32
U8 = mybir.dt.uint8
F8 = mybir.dt.float8_e4m3fn
X4 = mybir.dt.float8_e4m3fn_x4
ALU = mybir.AluOpType
ACT = mybir.ActivationFunctionType
Y_VECTOR = set()
EVAC_VECTOR = {(1, 1, 1), (1, 1, 3), (1, 0, 3)}

FLOPS = 2 * 2 * B * T * F * E


def tile_dpfpfastweightwriteread_kernel(tc, q, k, v_bytes, v_scale, beta, s0, gq, gs, out):
    nc = tc.nc

    with ExitStack() as ctx:
        const = ctx.enter_context(tc.tile_pool(name="const", bufs=1))
        loads = ctx.enter_context(tc.tile_pool(name="loads", bufs=1))
        work = ctx.enter_context(tc.tile_pool(name="work", bufs=2))
        small = ctx.enter_context(tc.tile_pool(name="small", bufs=4))
        outs = ctx.enter_context(tc.tile_pool(name="outs", bufs=8))
        zpool = ctx.enter_context(tc.tile_pool(name="zpool", bufs=3))
        codes = ctx.enter_context(tc.tile_pool(name="codes", bufs=3))
        psum_d = ctx.enter_context(tc.psum_pool(name="psum_d", bufs=1))
        psum_o = ctx.enter_context(tc.psum_pool(name="psum_o", bufs=2))
        psum_t = ctx.enter_context(tc.psum_pool(name="psum_t", bufs=2))

        x_t, xn_t, vb, s0r = {}, {}, {}, {}
        for b in range(B):
            for kind in ("k", "q"):
                x_t[kind, b] = loads.tile([P, G * J, A], BF16, name=f"x{kind}{b}")
                xn_t[kind, b] = loads.tile([P, G * J, A], BF16, name=f"xn{kind}{b}")

        def load_x(kind, b, g, r=0, n=J):
            src = k if kind == "k" else q
            rows = src[b].rearrange("(g p j) a -> g p (j a)", p=P, j=J)[g]
            c0, c1 = r * A, (r + n) * A
            x = x_t[kind, b][:].rearrange("p t a -> p (t a)")
            xs_ = xn_t[kind, b][:].rearrange("p t a -> p (t a)")
            o = g * J * A
            nc.sync.dma_start(out=x[:, o + c0 : o + c1], in_=rows[:, c0:c1])
            c2 = min(c1, J * A - 1)
            nc.sync.dma_start(out=xs_[:, o + c0 : o + c2], in_=rows[:, c0 + 1 : c2 + 1])

        def load_v(b, g):
            t = loads.tile([P, J, E], U8, name=f"vb{b}{g}")
            nc.sync.dma_start(out=t[:], in_=v_bytes[b].rearrange("(g p j) e -> g p j e", p=P, j=J)[g])
            vb[b, g] = t

        def load_s0(b):
            t = loads.tile([P, J, E], BF16, name=f"s0{b}")
            nc.sync.dma_start(out=t[:], in_=s0[b].rearrange("(p j) e -> p j e", j=J))
            s0r[b] = t

        beta_r = const.tile([P, B * G, J], BF16, name="beta_r")
        nc.scalar.dma_start(out=beta_r[:], in_=beta.rearrange("b t -> (b t)").rearrange("(n p j) -> p n j", p=P, j=J))
        vs_r = const.tile([P, G, J], F32, name="vs_r")
        nc.scalar.dma_start(out=vs_r[:], in_=v_scale.rearrange("o t u -> (o t u)").rearrange("(n p j) -> p n j", p=P, j=J))
        gs_r = const.tile([P, J], BF16, name="gs_r")
        nc.scalar.dma_start(out=gs_r[:], in_=gs.rearrange("(p j) -> p j", j=J))

        gq_t = const.tile([P, F], BF16, name="gq_t")
        for b in range(B):
            for g in range(G):
                if b + g == 0:
                    load_x("k", 0, 0, 0, 2)
                    load_v(0, 0)
                    load_x("k", 0, 0, 2, 2)
                else:
                    load_x("k", b, g)
                    load_v(b, g)
            load_s0(b)
            if b == 0:
                for g in range(G):
                    load_x("q", 0, g)
        for g in range(G):
            load_x("q", 1, g)
        nc.sync.dma_start(out=gq_t[:], in_=gq.partition_broadcast(P))

        ident = const.tile([P, P], F32, name="ident")
        make_identity(nc, ident[:])

        one = const.tile([P, 1], F32, name="one")
        nc.vector.memset(one[:], 1.0)
        eps = const.tile([P, 1], F32, name="eps")
        nc.vector.tensor_scalar(out=eps[:], in0=one[:], scalar1=1e-6, scalar2=None, op0=ALU.mult)
        warm = const.tile([P, 1], F32, name="warm")
        nc.scalar.activation(out=warm[:], in_=one[:], func=ACT.Abs_reciprocal_sqrt)
        absb = const.tile([P, B * G, J], F32, name="absb")
        nc.vector.scalar_tensor_tensor(out=absb[:], in0=beta_r[:], scalar=-1.0, in1=beta_r[:], op0=ALU.mult, op1=ALU.max)
        sgn = const.tile([P, B, G * J], F32, name="sgn")
        nc.vector.tensor_scalar(
            out=sgn[:].rearrange("p b (g j) -> p (b g) j", j=J),
            in0=beta_r[:],
            scalar1=0.0,
            scalar2=0.5,
            op0=ALU.is_ge,
            op1=ALU.subtract,
        )
        vss = const.tile([P, B, G * J], F32, name="vss")
        nc.vector.scalar_tensor_tensor(
            out=vss[:],
            in0=sgn[:],
            scalar=2.0,
            in1=vs_r[:].rearrange("p g j -> p (g j)").unsqueeze(1).to_broadcast([P, B, G * J]),
            op0=ALU.mult,
            op1=ALU.mult,
        )
        gs32 = const.tile([P, J], F32, name="gs32")
        nc.vector.tensor_scalar(out=gs32[:], in0=gs_r[:], scalar1=1.0 / 32.0, scalar2=None, op0=ALU.mult)
        g07 = const.tile([P, J], F32, name="g07")
        nc.vector.tensor_scalar(out=g07[:], in0=gs_r[:], scalar1=0.7, scalar2=None, op0=ALU.mult)
        gqn = const.tile([P, A], BF16, name="gqn")
        st = {}

        def cg():
            nc.gpsimd.tensor_scalar(out=gqn[:], in0=gq_t[:, A:F], scalar1=-1.0, scalar2=0.0, op0=ALU.mult, op1=ALU.add)

        def xn(kind, b, r, n):
            nc.gpsimd.tensor_scalar(
                out=xn_t[kind, b][:, r : r + n, A - 1 : A],
                in0=x_t[kind, b][:, r : r + n, 0:1],
                scalar1=-1.0,
                scalar2=0.0,
                op0=ALU.mult,
                op1=ALU.add,
            )

        def xw(kind, b, r, n):
            w = work.tile([P, n, A], BF16, name="w")
            nc.vector.scalar_tensor_tensor(
                out=w[:].rearrange("p t a -> p (t a)").bitcast(I32),
                in0=xn_t[kind, b][:, r : r + n, :].rearrange("p t a -> p (t a)").bitcast(I32),
                scalar=SIGNS,
                in1=x_t[kind, b][:, r : r + n, :].rearrange("p t a -> p (t a)").bitcast(I32),
                op0=ALU.bitwise_and,
                op1=ALU.bitwise_xor,
            )
            st["w", kind, b, r] = w

        def xz(kind, b, r, n):
            if ("z", kind, b) not in st:
                st["z", kind, b] = zpool.tile([P, G * J, A], F32, name="z")
                st["ss", kind, b] = small.tile([P, G * J], F32, name="ss")
                st["inv", kind, b] = small.tile([P, G * J], F32, name="inv")
            w, x, z = st["w", kind, b, r], x_t[kind, b][:, r : r + n, :], st["z", kind, b][:, r : r + n, :]
            for dst, src in ((slice(1, A), slice(0, A - 1)), (slice(0, 1), slice(A - 1, A))):
                nc.vector.scalar_tensor_tensor(
                    out=z[:, :, dst], in0=w[:, :, src], scalar=0.0, in1=x[:, :, dst], op0=ALU.max, op1=ALU.mult
                )

        def xs(kind, b, g):
            z, ss = st["z", kind, b], st["ss", kind, b]
            for t in range(g * J, (g + 1) * J):
                junk = small.tile([P, A], BF16, name="junk")
                nc.scalar.activation(out=junk[:], in_=z[:, t, :], func=ACT.Square, accum_out=ss[:, t : t + 1])

        def xr(kind, b, g, n):
            cols = slice(g * J, (g + n) * J)
            nc.scalar.activation(
                out=st["inv", kind, b][:, cols],
                in_=st["ss", kind, b][:, cols],
                func=ACT.Abs_reciprocal_sqrt,
                scale=1.0 / 512.0,
                bias=eps[:],
            )

        def xm(b, g, n):
            sk = small.tile([P, n * J], F32, name="sk")
            nc.gpsimd.tensor_tensor(
                out=sk[:],
                in0=st["inv", "k", b][:, g * J : (g + n) * J],
                in1=absb[:, b * G + g : b * G + g + n, :].rearrange("p n j -> p (n j)"),
                op=ALU.mult,
            )
            for m in range(n):
                st["sk", b, g + m] = sk[:, m * J : (m + 1) * J]

        def quantize(src, name, width):
            c = codes.tile([P, width], U32, align_bytes=64, name=name + "c")
            s = codes.tile([P, width], U8, align_bytes=64, name=name + "s")
            nc.vector.quantize_mx(out=c[:].bitcast(X4), scales=s[:], in_=src)
            return c, s

        def interleave(dst, src):
            nc.vector.tensor_copy(
                out=dst.rearrange("p (c i) t -> p c t i", i=4), in_=src.rearrange("p t (c i) -> p c t i", i=4)
            )

        def kz(b, g):
            z, sk = st["z", "k", b], st["sk", b, g]
            zs = work.tile([P, J, A], BF16, name="zs")
            for t in range(J):
                nc.scalar.activation(
                    out=zs[:, t, :].rearrange("p (j m) -> p j m", j=4),
                    in_=z[:, g * J + t, :].rearrange("p (m j) -> p j m", j=4),
                    func=ACT.Copy,
                    scale=sk[:, t : t + 1],
                )
            st["zs", b, g] = zs

        def ki(b, g):
            zi = work.tile([P, A, J], BF16, name="zi")
            interleave(zi[:], st["zs", b, g][:])
            st["zi", b, g] = zi

        def kh(b, g):
            kw = work.tile([P, F, J], BF16, align_bytes=64, name="kw")
            kwv = kw[:].rearrange("p (j h m) t -> p h j (m t)", j=4, h=2)
            ziv = st["zi", b, g][:].rearrange("p (j m) t -> p j (m t)", j=4)
            nc.vector.tensor_scalar(out=kwv[:, 0], in0=ziv, scalar1=0.0, scalar2=None, op0=ALU.max)
            nc.vector.tensor_scalar(out=kwv[:, 1], in0=ziv, scalar1=-1.0, scalar2=0.0, op0=ALU.mult, op1=ALU.max)
            st["kw", b, g] = kw

        def kq(b, g):
            st["kc", b, g] = quantize(st["kw", b, g][:].rearrange("p n t -> p (n t)"), "kw", GT)

        def vw(b, g):
            t_ = work.tile([P, J, E], BF16, name="vw")
            for t in range(J):
                nc.scalar.activation(
                    out=t_[:, t, :],
                    in_=vb[b, g][:, t, :].bitcast(F8),
                    func=ACT.Copy,
                    scale=vss[:, b, g * J + t : g * J + t + 1],
                )
            st["vw", b, g] = t_

        def vi(b, g):
            t_ = work.tile([P, E, J], BF16, align_bytes=64, name="vi")
            interleave(t_[:], st["vw", b, g][:])
            st["vi", b, g] = t_

        def vq(b, g):
            st["vc", b, g] = quantize(st["vi", b, g][:].rearrange("p n t -> p (n t)"), "v", GT)

        def wr(b, g):
            if g == 0:
                st["d", b] = [psum_d.tile([P, E], F32, name=f"d{j}") for j in range(4)]
            (kc, ks), (vc, vs) = st["kc", b, g], st["vc", b, g]
            for j in range(4):
                cols = slice(128 * j, 128 * (j + 1))
                nc.tensor.matmul_mx(
                    out=st["d", b][j][:],
                    lhsT=kc[:, cols].bitcast(X4),
                    lhsT_scale=ks[:, cols],
                    rhs=vc[:].bitcast(X4),
                    rhs_scale=vs[:],
                    start=(g == 0),
                    stop=(g == G - 1),
                )

        def sg(b):
            s0g = work.tile([P, 4, E], F32, name="s0g")
            for j in range(4):
                nc.scalar.activation(out=s0g[:, j, :], in_=s0r[b][:, j, :], func=ACT.Copy, scale=g07[:, j : j + 1])
            st["s0g", b] = s0g

        def sp(b):
            t_ = work.tile([P, 4, E], BF16, name="sp")
            for j in range(4):
                nc.vector.scalar_tensor_tensor(
                    out=t_[:, j, :],
                    in0=st["d", b][j][:],
                    scalar=gs32[:, j : j + 1],
                    in1=st["s0g", b][:, j, :],
                    op0=ALU.mult,
                    op1=ALU.add,
                )
            st["sp", b] = t_

        def si(b):
            t_ = work.tile([P, E, 4], BF16, align_bytes=64, name="si")
            interleave(t_[:], st["sp", b][:])
            st["si", b] = t_

        def sq(b):
            st["sc", b] = quantize(st["si", b][:].rearrange("p n t -> p (n t)"), "s", E)

        def qy(b, g):
            y = work.tile([P, J, A], F32, name="y")
            for t in range(J):
                n = g * J + t
                if (b, g) in Y_VECTOR:
                    nc.vector.tensor_scalar(
                        out=y[:, t, :],
                        in0=st["z", "q", b][:, n, :],
                        scalar1=st["inv", "q", b][:, n : n + 1],
                        scalar2=None,
                        op0=ALU.mult,
                    )
                else:
                    nc.scalar.activation(
                        out=y[:, t, :], in_=st["z", "q", b][:, n, :], func=ACT.Copy, scale=st["inv", "q", b][:, n : n + 1]
                    )
            st["y", b, g] = y

        def qg(b, g, t, n):
            if ("qf", b, g) not in st:
                st["qf", b, g] = work.tile([P, J, F], BF16, name="qf")
            for h, op, gain in ((0, ALU.max, gq_t[:, 0:A]), (1, ALU.min, gqn[:])):
                nc.vector.scalar_tensor_tensor(
                    out=st["qf", b, g][:, t : t + n, h * A : (h + 1) * A],
                    in0=st["y", b, g][:, t : t + n, :],
                    scalar=0.0,
                    in1=gain.unsqueeze(1).to_broadcast([P, n, A]),
                    op0=op,
                    op1=ALU.mult,
                )

        def qt(b, g, h):
            words = st["qf", b, g][:].bitcast(F32)
            tr = psum_t.tile([P, 2, 2, P], F32, name="tr")
            for a in range(2):
                for c in range(2):
                    nc.tensor.transpose(tr[:, a, c, :], words[:, 2 * h + a, c : F // 2 : 2], ident[:])
            st["tr", b, g, h] = tr

        def qe(b, g, h):
            if ("qw", b, g) not in st:
                st["qw", b, g] = work.tile([P, GT * 4], BF16, align_bytes=64, name="qw")
            nc.scalar.copy(
                out=st["qw", b, g][:].bitcast(F32)[:, h * GT : (h + 1) * GT].rearrange("p (a r c) -> p a r c", a=2, c=2),
                in_=st["tr", b, g, h][:].rearrange("p a c r -> p a r c"),
            )

        def qq(b, g, t, n):
            c, s = quantize(st["qw", b, g][:, t * 4 * P : (t + n) * 4 * P], "q", n * P)
            for m in range(n):
                cols = slice(m * P, (m + 1) * P)
                st["qc", b, g, t + m] = (c[:, cols], s[:, cols])

        def qo(b, g, t):
            (qc, qs), (sc, ss) = st["qc", b, g, t], st["sc", b]
            o = psum_o.tile([P, E], F32, name="o") if b == 0 else psum_d.tile([P, E], F32, name=f"d{t}")
            nc.tensor.matmul_mx(
                out=o[:],
                lhsT=qc.bitcast(X4),
                lhsT_scale=qs,
                rhs=sc[:].bitcast(X4),
                rhs_scale=ss[:],
                start=True,
                stop=True,
            )
            st["o", b, g, t] = o

        def oe(b, g, t):
            ot, o = outs.tile([P, E], F32, name="ot"), st["o", b, g, t]
            st["ot", b, g, t] = ot
            if (b, g, t) in EVAC_VECTOR:
                nc.vector.tensor_scalar(out=ot[:], in0=o[:], scalar1=512.0**-0.5, scalar2=None, op0=ALU.mult)
            else:
                nc.scalar.activation(out=ot[:], in_=o[:], func=ACT.Copy, scale=512.0**-0.5)

        def od(b, g, t):
            ov = out[b].rearrange("(g p j) e -> g p j e", p=P, j=J)[g]
            nc.sync.dma_start(out=ov[:, t, :], in_=st["ot", b, g, t][:])

        with tc.manual_schedule():
            xn("k", 0, 0, 2)
            xn("k", 0, 2, 2)
            xn("k", 0, 4, 4)
            xn("q", 0, 4, 4)
            xn("q", 0, 0, 4)
            xw("k", 0, 0, 2)
            xw("k", 0, 2, 2)
            xz("k", 0, 0, 2)
            xz("k", 0, 2, 2)
            xw("k", 0, 4, 4)
            vw(0, 0)
            vw(0, 1)
            vi(0, 0)
            xs("k", 0, 0)
            xr("k", 0, 0, 1)
            xn("k", 1, 0, 4)
            xm(0, 0, 1)
            xz("k", 0, 4, 4)
            xs("k", 0, 1)
            xn("k", 1, 4, 4)
            vi(0, 1)
            kz(0, 0)
            vq(0, 0)
            xw("q", 0, 0, 8)
            xr("k", 0, 1, 1)
            vw(1, 0)
            xm(0, 1, 1)
            vq(0, 1)
            xw("k", 1, 0, 8)
            xz("q", 0, 0, 8)
            ki(0, 0)
            xn("q", 1, 0, 4)
            kz(0, 1)
            xn("q", 1, 4, 4)
            xs("q", 0, 0)
            xz("k", 1, 0, 8)
            xs("q", 0, 1)
            xs("k", 1, 1)
            xr("q", 0, 0, 2)
            xs("k", 1, 0)
            kh(0, 0)
            xw("q", 1, 0, 8)
            kq(0, 0)
            wr(0, 0)
            ki(0, 1)
            xz("q", 1, 0, 8)
            qy(0, 1)
            kh(0, 1)
            vi(1, 0)
            kq(0, 1)
            wr(0, 1)
            cg()
            qg(0, 1, 0, 4)
            qy(0, 0)
            sg(0)
            xr("k", 1, 0, 2)
            xs("q", 1, 1)
            xs("q", 1, 0)
            xm(1, 0, 2)
            sp(0)
            kz(1, 0)
            qt(0, 1, 0)
            qe(0, 1, 0)
            qg(0, 0, 0, 4)
            xr("q", 1, 0, 2)
            ki(1, 0)
            qt(0, 1, 1)
            qe(0, 1, 1)
            qy(1, 1)
            kz(1, 1)
            si(0)
            vw(1, 1)
            vq(1, 0)
            qq(0, 1, 0, 4)
            qt(0, 0, 1)
            kh(1, 0)
            qt(0, 0, 0)
            qe(0, 0, 0)
            qe(0, 0, 1)
            sq(0)
            ki(1, 1)
            qo(0, 1, 2)
            qg(1, 1, 0, 2)
            qo(0, 1, 3)
            oe(0, 1, 2)
            kq(1, 0)
            oe(0, 1, 3)
            kh(1, 1)
            vi(1, 1)
            qy(1, 0)
            qq(0, 0, 0, 4)
            kq(1, 1)
            qt(1, 1, 0)
            sg(1)
            vq(1, 1)
            wr(1, 0)
            qo(0, 0, 3)
            qe(1, 1, 0)
            qo(0, 1, 0)
            oe(0, 1, 0)
            od(0, 1, 0)
            qg(1, 0, 0, 4)
            oe(0, 0, 3)
            wr(1, 1)
            qo(0, 0, 0)
            oe(0, 0, 0)
            sp(1)
            qt(1, 0, 0)
            qe(1, 0, 0)
            qo(0, 1, 1)
            od(0, 1, 3)
            oe(0, 1, 1)
            qo(0, 0, 1)
            qg(1, 1, 2, 2)
            si(1)
            qq(1, 1, 0, 2)
            qt(1, 0, 1)
            oe(0, 0, 1)
            qe(1, 0, 1)
            qo(0, 0, 2)
            oe(0, 0, 2)
            od(0, 0, 3)
            sq(1)
            od(0, 0, 1)
            od(0, 0, 0)
            qt(1, 1, 1)
            qe(1, 1, 1)
            qo(1, 1, 0)
            od(0, 1, 1)
            qo(1, 1, 1)
            qq(1, 0, 0, 4)
            oe(1, 1, 0)
            od(0, 1, 2)
            qq(1, 1, 2, 2)
            od(0, 0, 2)
            oe(1, 1, 1)
            od(1, 1, 0)
            qo(1, 0, 3)
            od(1, 1, 1)
            oe(1, 0, 3)
            qo(1, 0, 2)
            oe(1, 0, 2)
            od(1, 0, 3)
            qo(1, 0, 0)
            qo(1, 0, 1)
            oe(1, 0, 0)
            oe(1, 0, 1)
            od(1, 0, 2)
            od(1, 0, 0)
            od(1, 0, 1)
            qo(1, 1, 3)
            oe(1, 1, 3)
            qo(1, 1, 2)
            od(1, 1, 3)
            oe(1, 1, 2)
            od(1, 1, 2)
